import numpy as np
import ml_dtypes


def mxq(x, axis, fmt="e4m3"):
    dtype, down = {"e4m3": (ml_dtypes.float8_e4m3fn, 7), "e5m2": (ml_dtypes.float8_e5m2, 14)}[fmt]
    v = np.moveaxis(np.asarray(x, np.float32).astype(ml_dtypes.bfloat16).astype(np.float64), axis, -1)
    blocks = v.reshape(v.shape[:-1] + (-1, 32))
    amax = np.abs(blocks).max(-1, keepdims=True)
    byte = np.maximum(np.where(amax > 0, np.frexp(amax)[1] - 1 + 127, 0) - down, 1)
    scale = np.exp2(byte - 127.0)
    codes = (blocks / scale).astype(np.float32).astype(dtype).astype(np.float64)
    return np.moveaxis((codes * scale).reshape(v.shape), -1, axis)


WIDE = False


def mx_kscale(k):
    if not WIDE:
        return np.ones(k)
    levels = np.array([10, -10, 5, -5, 0])
    if k % 512:
        return np.exp2(np.random.permutation(np.resize(levels, k // 32))).repeat(32)
    a = np.empty((k // 512, 16))
    for p in range(k // 512):
        a[p, :8] = np.random.permutation(np.resize(levels, 8))
        for g in range(8):
            far = levels[np.abs(levels - a[p, g]) >= 10]
            a[p, g + 8] = far[np.random.randint(len(far))]
    return np.exp2(a.ravel()).repeat(32)


def f64(x):
    return np.asarray(x).astype(np.float64)


def striped(idx):
    return np.tile(idx.reshape(-1, 16).T, (8, 1)).astype(np.uint16)


def unstriped(offs):
    return offs[:16].T.reshape(-1).astype(np.int64)


E2M1 = np.array([0.0, 0.5, 1.0, 1.5, 2.0, 3.0, 4.0, 6.0, -0.0, -0.5, -1.0, -1.5, -2.0, -3.0, -4.0, -6.0])


def pack_weight(w, fmt):
    k, n = w.shape
    w = f64(np.asarray(w, np.float32).astype(ml_dtypes.bfloat16)).reshape(k // 32, 32, n)
    amax = np.abs(w).max(1)
    if fmt == "e4m3":
        byte = np.frexp(amax)[1] - 1 + 127 - 7
    else:
        mant, ex = np.frexp(amax / 6.0)
        byte = np.where(mant > 0.5, ex, ex - 1) + 127
    byte = np.clip(np.where(amax > 0, byte, 1), 1, 254)
    scaled = (w * np.exp2(127.0 - byte)[:, None, :]).reshape(k, n).astype(np.float32)
    by_word = np.ascontiguousarray(scaled.reshape(k // 512, 128, 4, n).transpose(0, 1, 3, 2))
    if fmt == "e4m3":
        words = by_word.astype(ml_dtypes.float8_e4m3fn).view(np.uint8)
    else:
        c = by_word.astype(ml_dtypes.float4_e2m1fn).view(np.uint8) & 0xF
        words = (c[..., 0::2] | (c[..., 1::2] << 4)).reshape(k // 512, 128, 2 * n)
    return np.ascontiguousarray(words), np.ascontiguousarray(byte.astype(np.uint8).reshape(k // 512, 16, n))


def unpack_weight(words, scales, fmt):
    g, _, n = scales.shape
    words = np.ascontiguousarray(words).reshape(g, 128, n, -1)
    if fmt == "e4m3":
        vals = words.view(ml_dtypes.float8_e4m3fn).astype(np.float64)
    else:
        nib = np.empty((g, 128, n, 4), np.uint8)
        nib[..., 0::2] = words & 0xF
        nib[..., 1::2] = words >> 4
        vals = E2M1[nib]
    vals = vals * np.repeat(np.exp2(scales.astype(np.float64) - 127.0), 8, axis=1)[..., None]
    return vals.transpose(0, 1, 3, 2).reshape(g * 512, n)


def gelu(v):
    return 0.5 * v * (1.0 + np.tanh(np.sqrt(2.0 / np.pi) * (v + 0.044715 * v**3)))


def bf(x):
    return np.asarray(x, np.float32).astype(ml_dtypes.bfloat16)

def planes(Y):
    n, m = Y.shape
    b = f64(bf(Y)).reshape(n // 32, 32, m)
    amax = np.abs(b).max(1)
    byte = np.clip(np.where(amax > 0, np.frexp(amax)[1] - 1 + 127 - 7, 1), 1, 254)
    codes = (b * np.exp2(127.0 - byte)[:, None, :]).reshape(n, m).astype(np.float32).astype(ml_dtypes.float8_e4m3fn).view(np.uint8)
    words = codes.reshape(n // 512, 128, 4, m).transpose(0, 1, 3, 2)
    return np.ascontiguousarray(words), np.ascontiguousarray(byte.astype(np.uint8).reshape(n // 512, 16, m))


K, T, H, S, T2, S2 = 2048, 4096, 512, 1024, 2048, 1024

def setup_inputs():
    n = np.random.standard_normal
    s = mx_kscale(K)[:, None]
    u = mx_kscale(H)[:, None]
    tab_words, tab_scales = pack_weight(n((K, T)) * s, "e4m3")
    tab2_words, tab2_scales = pack_weight(2.0 * n((H, T2)) / np.sqrt(H) / u, "e4m3")
    w4_words, w4_scales = pack_weight(1.5 * n((K, H)) / np.sqrt(K) / s, "e2m1")
    return {
        "tab_words": tab_words, "tab_scales": tab_scales,
        "tab2_words": tab2_words, "tab2_scales": tab2_scales,
        "w4_words": w4_words, "w4_scales": w4_scales,
        "w1": (n((K, H)) / np.sqrt(K) / s * u.T).astype(np.float32),
        "bn": (0.5 * n(S2)).astype(np.float32),
        "gain": np.exp(0.8 * n(S2)).astype(np.float32),
        "offs": striped(np.random.permutation(T)[:S]),
        "offs2": striped(np.random.permutation(T2)[:S2]),
    }

def reference(tab_words, tab_scales, tab2_words, tab2_scales, w4_words, w4_scales, w1, bn, gain, offs, offs2):
    v = unpack_weight(tab_words, tab_scales, "e4m3")[:, unstriped(offs)]
    v2 = unpack_weight(tab2_words, tab2_scales, "e4m3")[:, unstriped(offs2)]
    a = mxq(f64(w1), 0, "e4m3").T @ v
    b = unpack_weight(w4_words, w4_scales, "e2m1").T @ v
    h = a * (1.0 / (1.0 + np.exp(-b)))
    z = (v2.T @ mxq(h, 0, "e4m3")) + f64(bn)[:, None]
    act = 0.5 * z * (1.0 + np.tanh(0.7978845608028654 * (z + 0.044715 * z ** 3)))
    y = f64(gain)[:, None] * act
    words, scales = planes(y)
    return y, words, scales

@@ -1,0 +1,299 @@
+from contextlib import ExitStack
+
+import concourse.mybir as mybir
+
+K, T, H, S, T2, S2 = 2048, 4096, 512, 1024, 2048, 1024
+FLOPS = 2 * (2 * K * H * S + H * S2 * S)
+
+F32 = mybir.dt.float32
+BF16 = mybir.dt.bfloat16
+I32 = mybir.dt.int32
+U32 = mybir.dt.uint32
+U16 = mybir.dt.uint16
+U8 = mybir.dt.uint8
+FP8X4 = mybir.dt.float8_e4m3fn_x4
+FP4X4 = mybir.dt.float4_e2m1fn_x4
+ACT = mybir.ActivationFunctionType
+MULT = mybir.AluOpType.mult
+
+P = 128
+PACK = 4
+K_PASS = P * PACK
+PASSES = K // K_PASS
+GROUPS = S2 // K_PASS
+QUADS = 4
+QUAD = 32
+LIST_COLS = 16
+HALF = S // 2
+BANKS = 8
+TOK = S // BANKS
+BANK_F32 = 512
+CHUNK = 256
+CHUNKS = S // CHUNK
+SCALAR_GAINS = 2
+LAST_VECTOR = 40
+
+
+def tile_list_contextual_sparse_ffn_kernel(
+    tc, tab_words, tab_scales, tab2_words, tab2_scales, w4_words, w4_scales, w1, bn, gain, offs, offs2, out_0, out_1, out_2
+):
+    nc = tc.nc
+    with ExitStack() as ctx:
+        lists = ctx.enter_context(tc.tile_pool(name="lists", bufs=1))
+        keep = ctx.enter_context(tc.tile_pool(name="keep", bufs=1))
+        ring = ctx.enter_context(tc.tile_pool(name="ring", bufs=2))
+        psum = ctx.enter_context(tc.psum_pool(name="psum", bufs=1))
+
+        idx = lists.tile([P, S // LIST_COLS], U16, name="idx")
+        idx2 = lists.tile([P, S2 // LIST_COLS], U16, name="idx2")
+
+        with tc.tile_pool(name="tables", bufs=1) as tables:
+            region = T * 4
+            tab_sc = tables.tile([P, T], U8, name="tab_sc", offset=region)
+            w4_raw = tables.tile([P, PASSES, 2 * H], U8, name="w4_raw", offset=2 * region)
+            tab_w = [tables.tile([P, T], U32, name="tab_w%d" % a, offset=(a % 3) * region) for a in range(PASSES)]
+            w1_raw = [tables.tile([P, PACK, H], F32, name="w1_raw%d" % a, offset=region + a * region // 2) for a in range(PASSES - 1)]
+            w1_last = [
+                tables.tile([P, PACK, H // 2], F32, name="w1_last%d" % u, offset=region + (2 * (PASSES - 1) + u) * region // 4)
+                for u in range(2)
+            ]
+            w4_sc_raw = keep.tile([P, H], U8, name="w4_sc_raw", align_bytes=64)
+            tab2_sc = keep.tile([P, T2], U8, name="tab2_sc", align_bytes=64)
+            tab2_w = keep.tile([P, T2], U32, name="tab2_w", align_bytes=64)
+            planes = keep.tile([P, PASSES, S + H], U8, name="planes", align_bytes=64)
+            v2_plane = keep.tile([P, S2], U8, name="v2_plane", align_bytes=64)
+            bias = keep.tile([P, GROUPS, PACK], F32, name="bias")
+            gains = keep.tile([P, GROUPS, PACK], F32, name="gains")
+            rows = PACK * PASSES
+
+            def load_table(a):
+                nc.sync.dma_start(tab_w[a][:].bitcast(I32), tab_words[a].rearrange("p n i -> p (n i)").bitcast(I32))
+
+            def load_w1(a):
+                k_rows = w1[K_PASS * a : K_PASS * (a + 1), :].rearrange("(p j) c -> p j c", j=PACK)
+                if a < PASSES - 1:
+                    nc.sync.dma_start(w1_raw[a][:], k_rows)
+                else:
+                    for u in range(2):
+                        nc.sync.dma_start(w1_last[u][:], k_rows[:, :, u * H // 2 : (u + 1) * H // 2])
+
+            nc.sync.dma_start(idx[:], offs)
+            nc.sync.dma_start(tab_sc[QUAD : P - QUAD, :].bitcast(I32), tab_scales.rearrange("a q n -> q a n").bitcast(I32))
+            nc.sync.dma_start(w4_sc_raw[QUAD : P - QUAD, :].bitcast(I32), w4_scales.rearrange("a q n -> q a n").bitcast(I32))
+            nc.sync.dma_start(w4_raw[:].bitcast(I32), w4_words.rearrange("a p n -> p a n").bitcast(I32))
+            nc.sync.dma_start(idx2[:], offs2)
+            nc.sync.dma_start(tab2_sc[P - rows :, :].bitcast(I32), tab2_scales[0].bitcast(I32))
+            load_table(0)
+            nc.sync.dma_start(tab2_w[:].bitcast(I32), tab2_words[0].rearrange("p n i -> p (n i)").bitcast(I32))
+            nc.sync.dma_start(bias[:], bn.rearrange("(g p t) -> p g t", g=GROUPS, t=PACK))
+            nc.sync.dma_start(gains[:], gain.rearrange("(g p t) -> p g t", g=GROUPS, t=PACK))
+
+            for raw in (tab_sc, w4_sc_raw):
+                nc.vector.memset(raw[0:QUAD, :].bitcast(I32), 0)
+                nc.vector.memset(raw[P - QUAD :, :].bitcast(I32), 0)
+            nc.vector.memset(tab2_sc[0 : P - rows, :].bitcast(I32), 0)
+            nc.vector.memset(planes[:].bitcast(I32), 0)
+            nc.vector.memset(v2_plane[:].bitcast(I32), 0)
+
+            v_sc_picked = tables.tile([P, S], U8, name="v_sc_picked", offset=region + T)
+            staged = keep.tile([P, S + H], U8, name="staged", align_bytes=64)
+            nc.vector.tensor_copy(v_sc_picked[:], tab_sc[:].indirect(idx[:]))
+            nc.vector.tensor_copy(
+                staged[:, S:].rearrange("p (t m) -> p t m", t=PACK), w4_sc_raw[:].rearrange("p (m t) -> p t m", t=PACK)
+            )
+            nc.vector.tensor_copy(staged[:, 0:S].bitcast(I32), v_sc_picked[:].bitcast(I32))
+            for q in range(QUADS):
+                nc.sync.dma_start(
+                    planes[QUAD * q : QUAD * q + PACK, :, :].bitcast(I32),
+                    staged[QUAD + rows * q : QUAD + rows * (q + 1), :].bitcast(I32),
+                )
+            load_table(1)
+
+            w4_codes = [keep.tile([P, 2 * H], U8, name="w4_codes%d" % a, align_bytes=64) for a in range(PASSES)]
+            for a in range(PASSES):
+                nc.vector.tensor_copy(
+                    w4_codes[a][:].bitcast(U16).rearrange("p (t m) -> p t m", t=PACK),
+                    w4_raw[:, a, :].bitcast(U16).rearrange("p (m t) -> p t m", t=PACK),
+                )
+            load_table(2)
+
+            v2_picked = keep.tile([P, S2], U32, name="v2_picked", align_bytes=64)
+            v2_codes = keep.tile([P, S2], U32, name="v2_codes", align_bytes=64)
+            v2_sc_picked = keep.tile([P, S2], U8, name="v2_sc_picked", align_bytes=64)
+            v2_sc_dealt = keep.tile([P, S2], U8, name="v2_sc_dealt", align_bytes=64)
+            nc.vector.tensor_copy(v2_sc_picked[:], tab2_sc[:].indirect(idx2[:]))
+            nc.vector.tensor_copy(
+                v2_sc_dealt[:].rearrange("p (g t m) -> p g t m", g=GROUPS, t=PACK),
+                v2_sc_picked[:].rearrange("p (g m t) -> p g t m", g=GROUPS, t=PACK),
+            )
+            for q in range(QUADS):
+                nc.sync.dma_start(
+                    v2_plane[QUAD * q : QUAD * q + PACK, :].bitcast(I32),
+                    v2_sc_dealt[P - rows + PACK * q : P - rows + PACK * (q + 1), :].bitcast(I32),
+                )
+
+            v_codes = [
+                [keep.tile([P, HALF], U32, name="v_codes%d_%d" % (a, u), align_bytes=64) for u in range(2)] for a in range(PASSES)
+            ]
+
+            def product(bank, c, a, codes, w_plane, last):
+                u, n0 = divmod(c * TOK, HALF)
+                for t in range(PACK):
+                    nc.tensor.matmul_mx(
+                        out=bank[:, t, :],
+                        lhsT=codes(t),
+                        lhsT_scale=w_plane[:, P * t : P * (t + 1)],
+                        rhs=v_codes[a][u][:, n0 : n0 + TOK].bitcast(FP8X4),
+                        rhs_scale=planes[:, a, c * TOK : (c + 1) * TOK],
+                        start=(a == 0 and t == 0),
+                        stop=(a == last and t == PACK - 1),
+                    )
+
+            b_banks = [psum.tile([P, PACK, TOK], F32, name="b%d" % c, tag="bank%d" % c) for c in range(BANKS)]
+            half_cols = HALF // LIST_COLS
+            for a in range(PASSES):
+                for u in range(2):
+                    nc.vector.tensor_copy(v_codes[a][u][:], tab_w[a][:].indirect(idx[:, u * half_cols : (u + 1) * half_cols]))
+                if a == 0:
+                    load_table(3)
+                    nc.vector.tensor_copy(v2_picked[:], tab2_w[:].indirect(idx2[:]))
+                    nc.vector.tensor_copy(
+                        v2_codes[:].bitcast(I32).rearrange("p (g t b i) -> p g b t i", g=GROUPS, t=PACK, i=PACK),
+                        v2_picked[:].bitcast(I32).rearrange("p (g b i t) -> p g b t i", g=GROUPS, t=PACK, i=PACK),
+                    )
+                if a in (1, 2):
+                    load_w1(2 * a - 2)
+                    load_w1(2 * a - 1)
+                for c in range(BANKS):
+                    product(
+                        b_banks[c], c, a, lambda t: w4_codes[a][:, 2 * P * t : 2 * P * (t + 1)].bitcast(FP4X4), planes[:, a, S:], PASSES - 1
+                    )
+
+            gates = [keep.tile([P, TOK, PACK], F32, name="gate%d" % c) for c in range(BANKS)]
+            for c in range(BANKS):
+                nc.scalar.activation(gates[c][:], b_banks[c][:].rearrange("p t n -> p n t"), ACT.Sigmoid)
+
+            w1_codes = [keep.tile([P, H], U32, name="w1_codes%d" % a, align_bytes=64) for a in range(PASSES)]
+            w1_planes = [keep.tile([P, H], U8, name="w1_plane%d" % a, align_bytes=64) for a in range(PASSES)]
+            for a in range(PASSES):
+                w1_bf = ring.tile([P, H * PACK], BF16, name="w1_bf", align_bytes=64)
+                dealt = w1_bf[:].rearrange("p (t m j) -> p m t j", t=PACK, j=PACK)
+                if a < PASSES - 1:
+                    nc.vector.tensor_copy(dealt, w1_raw[a][:].rearrange("p j (m t) -> p m t j", t=PACK))
+                    nc.vector.quantize_mx(out=w1_codes[a][:].bitcast(FP8X4), scales=w1_planes[a][:], in_=w1_bf[:])
+                else:
+                    halves = [w1_last[u][:].rearrange("p j (m t) -> p m t j", t=PACK) for u in range(2)]
+                    mid = P // 2
+                    nc.vector.tensor_copy(dealt[:, 0:mid], halves[0])
+                    nc.vector.tensor_copy(dealt[:, mid : mid + LAST_VECTOR], halves[1][:, 0:LAST_VECTOR])
+                    nc.scalar.copy(dealt[:, mid + LAST_VECTOR :], halves[1][:, LAST_VECTOR:])
+                    for u in range(2):
+                        cols = slice(u * H // 2, (u + 1) * H // 2)
+                        nc.vector.quantize_mx(
+                            out=w1_codes[a][:, cols].bitcast(FP8X4),
+                            scales=w1_planes[a][:, cols],
+                            in_=w1_bf[:, u * H * PACK // 2 : (u + 1) * H * PACK // 2],
+                        )
+
+        late = ctx.enter_context(tc.tile_pool(name="late", bufs=1))
+        a_banks = [psum.tile([P, PACK, TOK], F32, name="a%d" % c, tag="bank%d" % c) for c in range(BANKS)]
+
+        def project(a, banks):
+            for c in banks:
+                product(a_banks[c], c, a, lambda t: w1_codes[a][:, P * t : P * (t + 1)].bitcast(FP8X4), w1_planes[a][:], stop_pass[c])
+
+        per_chunk = CHUNK // TOK
+        stop_pass = [PASSES - 1 if c < per_chunk else PASSES - 2 for c in range(BANKS)]
+
+        def close_projection(ci):
+            banks = range(ci * per_chunk, (ci + 1) * per_chunk)
+            for a in (2, 3) if ci == 0 else (3, 2):
+                project(a, banks)
+
+        h_codes, h_planes = {}, {}
+
+        def make_h(ci):
+            h_bf = late.tile([P, CHUNK * PACK], BF16, name="h_bf%d" % ci, align_bytes=64)
+            for s in range(per_chunk):
+                c = ci * per_chunk + s
+                nc.vector.tensor_tensor(
+                    h_bf[:, s * TOK * PACK : (s + 1) * TOK * PACK].rearrange("p (n t) -> p n t", t=PACK),
+                    a_banks[c][:].rearrange("p t n -> p n t"),
+                    gates[c][:],
+                    MULT,
+                )
+            h_codes[ci] = late.tile([P, CHUNK], U32, name="h_codes%d" % ci, align_bytes=64)
+            h_planes[ci] = late.tile([P, CHUNK], U8, name="h_plane%d" % ci, align_bytes=64)
+            nc.vector.quantize_mx(out=h_codes[ci][:].bitcast(FP8X4), scales=h_planes[ci][:], in_=h_bf[:])
+
+        y_planes = late.tile([P, GROUPS, S], U8, name="y_planes", align_bytes=64)
+        per_bank = BANK_F32 // CHUNK
+        ys = {}
+
+        def scalar_gains(ci, g):
+            if ci == 0:
+                return PACK
+            if (ci, g) == (CHUNKS - 1, GROUPS - 1):
+                return 0
+            return SCALAR_GAINS
+
+        def neurons(ci, g):
+            y = late.tile([P, PACK, CHUNK], F32, name="y%d_%d" % (ci, g), align_bytes=64)
+            ys[ci, g] = y
+            for t0 in range(0, PACK, per_bank):
+                bank = (g * PACK + t0) // per_bank
+                z = psum.tile([P, per_bank, CHUNK], F32, name="z%d_%d" % (ci, bank), tag="bank%d" % bank)
+                for s in range(per_bank):
+                    col = K_PASS * g + P * (t0 + s)
+                    nc.tensor.matmul_mx(
+                        out=z[:, s, :],
+                        lhsT=v2_codes[:, col : col + P].bitcast(FP8X4),
+                        lhsT_scale=v2_plane[:, col : col + P],
+                        rhs=h_codes[ci][:].bitcast(FP8X4),
+                        rhs_scale=h_planes[ci][:],
+                        start=True,
+                        stop=True,
+                    )
+                for s in range(per_bank):
+                    t = t0 + s
+                    nc.scalar.activation(y[:, t, :], z[:, s, :], ACT.Gelu_apprx_tanh, bias=bias[:, g, t : t + 1])
+            for t in range(scalar_gains(ci, g)):
+                nc.scalar.activation(y[:, t, :], y[:, t, :], ACT.Copy, scale=gains[:, g, t : t + 1])
+
+        def hand_out(ci, g):
+            y = ys[ci, g]
+            m0 = ci * CHUNK
+            for t in range(scalar_gains(ci, g), PACK):
+                nc.vector.tensor_scalar(y[:, t, :], y[:, t, :], gains[:, g, t : t + 1], None, MULT)
+            nc.sync.dma_start(out_0[K_PASS * g : K_PASS * (g + 1), m0 : m0 + CHUNK].rearrange("(p t) m -> p t m", t=PACK), y[:])
+            y_bf = ring.tile([P, CHUNK * PACK], BF16, name="y_bf", align_bytes=64)
+            nc.vector.tensor_copy(
+                y_bf[:].rearrange("p (b i t) -> p b t i", t=PACK, i=PACK),
+                y[:].rearrange("p t (b i) -> p b t i", i=PACK),
+            )
+            y_codes = late.tile([P, CHUNK], U32, name="y_codes%d_%d" % (ci, g), align_bytes=64)
+            nc.vector.quantize_mx(out=y_codes[:].bitcast(FP8X4), scales=y_planes[:, g, m0 : m0 + CHUNK], in_=y_bf[:])
+            nc.sync.dma_start(
+                out_1[g].rearrange("p m t -> p (m t)")[:, PACK * m0 : PACK * (m0 + CHUNK)].bitcast(I32),
+                y_codes[:].bitcast(I32),
+            )
+
+        project(0, range(BANKS))
+        project(1, range(BANKS))
+        close_projection(0)
+        close_projection(1)
+        make_h(0)
+        for ci in range(CHUNKS):
+            neurons(ci, 0)
+            if ci + 1 < CHUNKS:
+                make_h(ci + 1)
+            if ci + 2 < CHUNKS:
+                close_projection(ci + 2)
+            neurons(ci, 1)
+            hand_out(ci, 0)
+            hand_out(ci, 1)
+        for q in range(QUADS):
+            nc.scalar.dma_start(
+                out_2[:, PACK * q : PACK * (q + 1), :].rearrange("g r m -> r g m").bitcast(I32),
+                y_planes[QUAD * q : QUAD * q + PACK, :, :].bitcast(I32),
+            )

@@ -28,9 +28,10 @@ HALF = S // 2
 BANKS = 8
 TOK = S // BANKS
 BANK_F32 = 512
-CHUNK = 256
-CHUNKS = S // CHUNK
-SCALAR_GAINS = 2
+PIECE = 256
+STORE_COLS = 1024
+CHUNKS = [256, 512, 256]
+SCALAR_GAINS = [4, 1, 0]
 LAST_VECTOR = 40
 
 
@@ -41,159 +42,165 @@ def tile_list_contextual_sparse_ffn_kernel(
     with ExitStack() as ctx:
         lists = ctx.enter_context(tc.tile_pool(name="lists", bufs=1))
         keep = ctx.enter_context(tc.tile_pool(name="keep", bufs=1))
-        ring = ctx.enter_context(tc.tile_pool(name="ring", bufs=2))
+        ring = ctx.enter_context(tc.tile_pool(name="ring", bufs=3))
         psum = ctx.enter_context(tc.psum_pool(name="psum", bufs=1))
 
         idx = lists.tile([P, S // LIST_COLS], U16, name="idx")
         idx2 = lists.tile([P, S2 // LIST_COLS], U16, name="idx2")
 
-        with tc.tile_pool(name="tables", bufs=1) as tables:
-            region = T * 4
-            tab_sc = tables.tile([P, T], U8, name="tab_sc", offset=region)
-            w4_raw = tables.tile([P, PASSES, 2 * H], U8, name="w4_raw", offset=2 * region)
-            tab_w = [tables.tile([P, T], U32, name="tab_w%d" % a, offset=(a % 3) * region) for a in range(PASSES)]
-            w1_raw = [tables.tile([P, PACK, H], F32, name="w1_raw%d" % a, offset=region + a * region // 2) for a in range(PASSES - 1)]
-            w1_last = [
-                tables.tile([P, PACK, H // 2], F32, name="w1_last%d" % u, offset=region + (2 * (PASSES - 1) + u) * region // 4)
-                for u in range(2)
-            ]
-            w4_sc_raw = keep.tile([P, H], U8, name="w4_sc_raw", align_bytes=64)
-            tab2_sc = keep.tile([P, T2], U8, name="tab2_sc", align_bytes=64)
-            tab2_w = keep.tile([P, T2], U32, name="tab2_w", align_bytes=64)
-            planes = keep.tile([P, PASSES, S + H], U8, name="planes", align_bytes=64)
-            v2_plane = keep.tile([P, S2], U8, name="v2_plane", align_bytes=64)
-            bias = keep.tile([P, GROUPS, PACK], F32, name="bias")
-            gains = keep.tile([P, GROUPS, PACK], F32, name="gains")
-            rows = PACK * PASSES
+        tables = ctx.enter_context(tc.tile_pool(name="tables", bufs=1))
+        region = T * 4
+        tab_sc = tables.tile([P, T], U8, name="tab_sc", offset=region)
+        w4_raw = tables.tile([P, PASSES, 2 * H], U8, name="w4_raw", offset=2 * region)
+        tab_w = [tables.tile([P, T], U32, name="tab_w%d" % a, offset=(a % 3) * region) for a in range(PASSES)]
+        w1_raw = [tables.tile([P, PACK, H], F32, name="w1_raw%d" % a, offset=region + a * region // 2) for a in range(PASSES - 1)]
+        w1_last = [
+            tables.tile([P, PACK, H // 2], F32, name="w1_last%d" % u, offset=region + (2 * (PASSES - 1) + u) * region // 4)
+            for u in range(2)
+        ]
+        w4_sc_raw = keep.tile([P, H], U8, name="w4_sc_raw", align_bytes=64)
+        tab2_sc = keep.tile([P, T2], U8, name="tab2_sc", align_bytes=64)
+        tab2_w = keep.tile([P, T2], U32, name="tab2_w", align_bytes=64)
+        planes = keep.tile([P, PASSES, S + H], U8, name="planes", align_bytes=64)
+        v2_plane = tables.tile([P, S2], U8, name="v2_plane", offset=0, align_bytes=64)
+        bias = tables.tile([P, GROUPS, PACK], F32, name="bias", offset=S2)
+        gains = tables.tile([P, GROUPS, PACK], F32, name="gains", offset=S2 + 64)
+        rows = PACK * PASSES
 
-            def load_table(a):
-                nc.sync.dma_start(tab_w[a][:].bitcast(I32), tab_words[a].rearrange("p n i -> p (n i)").bitcast(I32))
+        def load_table(a):
+            nc.sync.dma_start(tab_w[a][:].bitcast(I32), tab_words[a].rearrange("p n i -> p (n i)").bitcast(I32))
 
-            def load_w1(a):
-                k_rows = w1[K_PASS * a : K_PASS * (a + 1), :].rearrange("(p j) c -> p j c", j=PACK)
-                if a < PASSES - 1:
-                    nc.sync.dma_start(w1_raw[a][:], k_rows)
-                else:
-                    for u in range(2):
-                        nc.sync.dma_start(w1_last[u][:], k_rows[:, :, u * H // 2 : (u + 1) * H // 2])
-
-            nc.sync.dma_start(idx[:], offs)
-            nc.sync.dma_start(tab_sc[QUAD : P - QUAD, :].bitcast(I32), tab_scales.rearrange("a q n -> q a n").bitcast(I32))
-            nc.sync.dma_start(w4_sc_raw[QUAD : P - QUAD, :].bitcast(I32), w4_scales.rearrange("a q n -> q a n").bitcast(I32))
-            nc.sync.dma_start(w4_raw[:].bitcast(I32), w4_words.rearrange("a p n -> p a n").bitcast(I32))
-            nc.sync.dma_start(idx2[:], offs2)
-            nc.sync.dma_start(tab2_sc[P - rows :, :].bitcast(I32), tab2_scales[0].bitcast(I32))
-            load_table(0)
-            nc.sync.dma_start(tab2_w[:].bitcast(I32), tab2_words[0].rearrange("p n i -> p (n i)").bitcast(I32))
-            nc.sync.dma_start(bias[:], bn.rearrange("(g p t) -> p g t", g=GROUPS, t=PACK))
-            nc.sync.dma_start(gains[:], gain.rearrange("(g p t) -> p g t", g=GROUPS, t=PACK))
-
-            for raw in (tab_sc, w4_sc_raw):
-                nc.vector.memset(raw[0:QUAD, :].bitcast(I32), 0)
-                nc.vector.memset(raw[P - QUAD :, :].bitcast(I32), 0)
-            nc.vector.memset(tab2_sc[0 : P - rows, :].bitcast(I32), 0)
-            nc.vector.memset(planes[:].bitcast(I32), 0)
-            nc.vector.memset(v2_plane[:].bitcast(I32), 0)
-
-            v_sc_picked = tables.tile([P, S], U8, name="v_sc_picked", offset=region + T)
-            staged = keep.tile([P, S + H], U8, name="staged", align_bytes=64)
-            nc.vector.tensor_copy(v_sc_picked[:], tab_sc[:].indirect(idx[:]))
-            nc.vector.tensor_copy(
-                staged[:, S:].rearrange("p (t m) -> p t m", t=PACK), w4_sc_raw[:].rearrange("p (m t) -> p t m", t=PACK)
-            )
-            nc.vector.tensor_copy(staged[:, 0:S].bitcast(I32), v_sc_picked[:].bitcast(I32))
-            for q in range(QUADS):
-                nc.sync.dma_start(
-                    planes[QUAD * q : QUAD * q + PACK, :, :].bitcast(I32),
-                    staged[QUAD + rows * q : QUAD + rows * (q + 1), :].bitcast(I32),
-                )
-            load_table(1)
-
-            w4_codes = [keep.tile([P, 2 * H], U8, name="w4_codes%d" % a, align_bytes=64) for a in range(PASSES)]
-            for a in range(PASSES):
-                nc.vector.tensor_copy(
-                    w4_codes[a][:].bitcast(U16).rearrange("p (t m) -> p t m", t=PACK),
-                    w4_raw[:, a, :].bitcast(U16).rearrange("p (m t) -> p t m", t=PACK),
-                )
-            load_table(2)
-
-            v2_picked = keep.tile([P, S2], U32, name="v2_picked", align_bytes=64)
-            v2_codes = keep.tile([P, S2], U32, name="v2_codes", align_bytes=64)
-            v2_sc_picked = keep.tile([P, S2], U8, name="v2_sc_picked", align_bytes=64)
-            v2_sc_dealt = keep.tile([P, S2], U8, name="v2_sc_dealt", align_bytes=64)
-            nc.vector.tensor_copy(v2_sc_picked[:], tab2_sc[:].indirect(idx2[:]))
-            nc.vector.tensor_copy(
-                v2_sc_dealt[:].rearrange("p (g t m) -> p g t m", g=GROUPS, t=PACK),
-                v2_sc_picked[:].rearrange("p (g m t) -> p g t m", g=GROUPS, t=PACK),
-            )
-            for q in range(QUADS):
-                nc.sync.dma_start(
-                    v2_plane[QUAD * q : QUAD * q + PACK, :].bitcast(I32),
-                    v2_sc_dealt[P - rows + PACK * q : P - rows + PACK * (q + 1), :].bitcast(I32),
-                )
-
-            v_codes = [
-                [keep.tile([P, HALF], U32, name="v_codes%d_%d" % (a, u), align_bytes=64) for u in range(2)] for a in range(PASSES)
-            ]
-
-            def product(bank, c, a, codes, w_plane, last):
-                u, n0 = divmod(c * TOK, HALF)
-                for t in range(PACK):
-                    nc.tensor.matmul_mx(
-                        out=bank[:, t, :],
-                        lhsT=codes(t),
-                        lhsT_scale=w_plane[:, P * t : P * (t + 1)],
-                        rhs=v_codes[a][u][:, n0 : n0 + TOK].bitcast(FP8X4),
-                        rhs_scale=planes[:, a, c * TOK : (c + 1) * TOK],
-                        start=(a == 0 and t == 0),
-                        stop=(a == last and t == PACK - 1),
-                    )
-
-            b_banks = [psum.tile([P, PACK, TOK], F32, name="b%d" % c, tag="bank%d" % c) for c in range(BANKS)]
-            half_cols = HALF // LIST_COLS
-            for a in range(PASSES):
+        def load_w1(a):
+            k_rows = w1[K_PASS * a : K_PASS * (a + 1), :].rearrange("(p j) c -> p j c", j=PACK)
+            if a < PASSES - 1:
+                nc.sync.dma_start(w1_raw[a][:], k_rows)
+            else:
                 for u in range(2):
-                    nc.vector.tensor_copy(v_codes[a][u][:], tab_w[a][:].indirect(idx[:, u * half_cols : (u + 1) * half_cols]))
-                if a == 0:
-                    load_table(3)
-                    nc.vector.tensor_copy(v2_picked[:], tab2_w[:].indirect(idx2[:]))
-                    nc.vector.tensor_copy(
-                        v2_codes[:].bitcast(I32).rearrange("p (g t b i) -> p g b t i", g=GROUPS, t=PACK, i=PACK),
-                        v2_picked[:].bitcast(I32).rearrange("p (g b i t) -> p g b t i", g=GROUPS, t=PACK, i=PACK),
-                    )
-                if a in (1, 2):
-                    load_w1(2 * a - 2)
-                    load_w1(2 * a - 1)
-                for c in range(BANKS):
-                    product(
-                        b_banks[c], c, a, lambda t: w4_codes[a][:, 2 * P * t : 2 * P * (t + 1)].bitcast(FP4X4), planes[:, a, S:], PASSES - 1
-                    )
+                    nc.sync.dma_start(w1_last[u][:], k_rows[:, :, u * H // 2 : (u + 1) * H // 2])
 
-            gates = [keep.tile([P, TOK, PACK], F32, name="gate%d" % c) for c in range(BANKS)]
+        nc.sync.dma_start(idx[:], offs)
+        nc.sync.dma_start(tab_sc[QUAD : P - QUAD, :].bitcast(I32), tab_scales.rearrange("a q n -> q a n").bitcast(I32))
+        nc.sync.dma_start(w4_sc_raw[QUAD : P - QUAD, :].bitcast(I32), w4_scales.rearrange("a q n -> q a n").bitcast(I32))
+        nc.sync.dma_start(w4_raw[:].bitcast(I32), w4_words.rearrange("a p n -> p a n").bitcast(I32))
+        nc.sync.dma_start(idx2[:], offs2)
+        nc.sync.dma_start(tab2_sc[P - rows :, :].bitcast(I32), tab2_scales[0].bitcast(I32))
+        load_table(0)
+        nc.sync.dma_start(tab2_w[:].bitcast(I32), tab2_words[0].rearrange("p n i -> p (n i)").bitcast(I32))
+
+        for raw in (tab_sc, w4_sc_raw):
+            nc.vector.memset(raw[0:QUAD, :].bitcast(I32), 0)
+            nc.vector.memset(raw[P - QUAD :, :].bitcast(I32), 0)
+        nc.vector.memset(tab2_sc[0 : P - rows, :].bitcast(I32), 0)
+        nc.vector.memset(planes[:].bitcast(I32), 0)
+
+        v_sc_picked = tables.tile([P, S], U8, name="v_sc_picked", offset=region + T)
+        staged = keep.tile([P, S + H], U8, name="staged", align_bytes=64)
+        nc.vector.tensor_copy(v_sc_picked[:], tab_sc[:].indirect(idx[:]))
+        nc.vector.tensor_copy(
+            staged[:, S:].rearrange("p (t m) -> p t m", t=PACK), w4_sc_raw[:].rearrange("p (m t) -> p t m", t=PACK)
+        )
+        nc.vector.tensor_copy(staged[:, 0:S].bitcast(I32), v_sc_picked[:].bitcast(I32))
+        for q in range(QUADS):
+            nc.sync.dma_start(
+                planes[QUAD * q : QUAD * q + PACK, :, :].bitcast(I32),
+                staged[QUAD + rows * q : QUAD + rows * (q + 1), :].bitcast(I32),
+            )
+        load_table(1)
+
+        w4_codes = [keep.tile([P, 2 * H], U8, name="w4_codes%d" % a, align_bytes=64) for a in range(PASSES)]
+        for a in range(PASSES):
+            nc.vector.tensor_copy(
+                w4_codes[a][:].bitcast(U16).rearrange("p (t m) -> p t m", t=PACK),
+                w4_raw[:, a, :].bitcast(U16).rearrange("p (m t) -> p t m", t=PACK),
+            )
+        load_table(2)
+
+        v2_picked = keep.tile([P, S2], U32, name="v2_picked", align_bytes=64)
+        v2_codes = keep.tile([P, S2], U32, name="v2_codes", align_bytes=64)
+        v2_sc_picked = keep.tile([P, S2], U8, name="v2_sc_picked", align_bytes=64)
+        v2_sc_dealt = keep.tile([P, S2], U8, name="v2_sc_dealt", align_bytes=64)
+        nc.vector.tensor_copy(v2_sc_picked[:], tab2_sc[:].indirect(idx2[:]))
+        nc.vector.tensor_copy(
+            v2_sc_dealt[:].rearrange("p (g t m) -> p g t m", g=GROUPS, t=PACK),
+            v2_sc_picked[:].rearrange("p (g m t) -> p g t m", g=GROUPS, t=PACK),
+        )
+
+        v_codes = [
+            [keep.tile([P, HALF], U32, name="v_codes%d_%d" % (a, u), align_bytes=64) for u in range(2)] for a in range(PASSES)
+        ]
+
+        def product(bank, c, a, codes, w_plane, last):
+            u, n0 = divmod(c * TOK, HALF)
+            for t in range(PACK):
+                nc.tensor.matmul_mx(
+                    out=bank[:, t, :],
+                    lhsT=codes(t),
+                    lhsT_scale=w_plane[:, P * t : P * (t + 1)],
+                    rhs=v_codes[a][u][:, n0 : n0 + TOK].bitcast(FP8X4),
+                    rhs_scale=planes[:, a, c * TOK : (c + 1) * TOK],
+                    start=(a == 0 and t == 0),
+                    stop=(a == last and t == PACK - 1),
+                )
+
+        b_banks = [psum.tile([P, PACK, TOK], F32, name="b%d" % c, tag="bank%d" % c) for c in range(BANKS)]
+        half_cols = HALF // LIST_COLS
+        for a in range(PASSES):
+            for u in range(2):
+                nc.vector.tensor_copy(v_codes[a][u][:], tab_w[a][:].indirect(idx[:, u * half_cols : (u + 1) * half_cols]))
+            if a == 0:
+                load_table(3)
+                nc.vector.tensor_copy(v2_picked[:], tab2_w[:].indirect(idx2[:]))
+                nc.vector.tensor_copy(
+                    v2_codes[:].bitcast(I32).rearrange("p (g t b i) -> p g b t i", g=GROUPS, t=PACK, i=PACK),
+                    v2_picked[:].bitcast(I32).rearrange("p (g b i t) -> p g b t i", g=GROUPS, t=PACK, i=PACK),
+                )
+            if a in (1, 2):
+                load_w1(2 * a - 2)
+                load_w1(2 * a - 1)
             for c in range(BANKS):
-                nc.scalar.activation(gates[c][:], b_banks[c][:].rearrange("p t n -> p n t"), ACT.Sigmoid)
+                product(
+                    b_banks[c], c, a, lambda t: w4_codes[a][:, 2 * P * t : 2 * P * (t + 1)].bitcast(FP4X4), planes[:, a, S:], PASSES - 1
+                )
 
-            w1_codes = [keep.tile([P, H], U32, name="w1_codes%d" % a, align_bytes=64) for a in range(PASSES)]
-            w1_planes = [keep.tile([P, H], U8, name="w1_plane%d" % a, align_bytes=64) for a in range(PASSES)]
-            for a in range(PASSES):
-                w1_bf = ring.tile([P, H * PACK], BF16, name="w1_bf", align_bytes=64)
-                dealt = w1_bf[:].rearrange("p (t m j) -> p m t j", t=PACK, j=PACK)
-                if a < PASSES - 1:
-                    nc.vector.tensor_copy(dealt, w1_raw[a][:].rearrange("p j (m t) -> p m t j", t=PACK))
-                    nc.vector.quantize_mx(out=w1_codes[a][:].bitcast(FP8X4), scales=w1_planes[a][:], in_=w1_bf[:])
+        nc.vector.memset(v2_plane[:].bitcast(I32), 0)
+        for q in range(QUADS):
+            nc.sync.dma_start(
+                v2_plane[QUAD * q : QUAD * q + PACK, :].bitcast(I32),
+                v2_sc_dealt[P - rows + PACK * q : P - rows + PACK * (q + 1), :].bitcast(I32),
+            )
+        nc.sync.dma_start(bias[:], bn.rearrange("(g p t) -> p g t", g=GROUPS, t=PACK))
+        nc.sync.dma_start(gains[:], gain.rearrange("(g p t) -> p g t", g=GROUPS, t=PACK))
+
+        gates = [keep.tile([P, TOK, PACK], F32, name="gate%d" % c) for c in range(BANKS)]
+        for c in range(BANKS):
+            nc.scalar.activation(gates[c][:], b_banks[c][:].rearrange("p t n -> p n t"), ACT.Sigmoid)
+
+        w1_codes = [keep.tile([P, H], U32, name="w1_codes%d" % a, align_bytes=64) for a in range(PASSES)]
+        w1_planes = [keep.tile([P, H], U8, name="w1_plane%d" % a, align_bytes=64) for a in range(PASSES)]
+        for a in range(PASSES):
+            w1_bf = ring.tile([P, H * PACK], BF16, name="w1_bf", align_bytes=64)
+            dealt = w1_bf[:].rearrange("p (t m j) -> p m t j", t=PACK, j=PACK)
+            if a < PASSES - 1:
+                whole = w1_raw[a][:].rearrange("p j (m t) -> p m t j", t=PACK)
+                if a < PASSES - 2:
+                    nc.vector.tensor_copy(dealt, whole)
                 else:
-                    halves = [w1_last[u][:].rearrange("p j (m t) -> p m t j", t=PACK) for u in range(2)]
-                    mid = P // 2
-                    nc.vector.tensor_copy(dealt[:, 0:mid], halves[0])
-                    nc.vector.tensor_copy(dealt[:, mid : mid + LAST_VECTOR], halves[1][:, 0:LAST_VECTOR])
-                    nc.scalar.copy(dealt[:, mid + LAST_VECTOR :], halves[1][:, LAST_VECTOR:])
-                    for u in range(2):
-                        cols = slice(u * H // 2, (u + 1) * H // 2)
-                        nc.vector.quantize_mx(
-                            out=w1_codes[a][:, cols].bitcast(FP8X4),
-                            scales=w1_planes[a][:, cols],
-                            in_=w1_bf[:, u * H * PACK // 2 : (u + 1) * H * PACK // 2],
-                        )
+                    nc.vector.tensor_copy(dealt[:, 0 : 2 * LAST_VECTOR], whole[:, 0 : 2 * LAST_VECTOR])
+                    nc.scalar.copy(dealt[:, 2 * LAST_VECTOR :], whole[:, 2 * LAST_VECTOR :])
+                nc.vector.quantize_mx(out=w1_codes[a][:].bitcast(FP8X4), scales=w1_planes[a][:], in_=w1_bf[:])
+            else:
+                halves = [w1_last[u][:].rearrange("p j (m t) -> p m t j", t=PACK) for u in range(2)]
+                mid = P // 2
+                nc.vector.tensor_copy(dealt[:, 0:mid], halves[0])
+                nc.vector.tensor_copy(dealt[:, mid : mid + LAST_VECTOR], halves[1][:, 0:LAST_VECTOR])
+                nc.scalar.copy(dealt[:, mid + LAST_VECTOR :], halves[1][:, LAST_VECTOR:])
+                for u in range(2):
+                    cols = slice(u * H // 2, (u + 1) * H // 2)
+                    nc.vector.quantize_mx(
+                        out=w1_codes[a][:, cols].bitcast(FP8X4),
+                        scales=w1_planes[a][:, cols],
+                        in_=w1_bf[:, u * H * PACK // 2 : (u + 1) * H * PACK // 2],
+                    )
 
         late = ctx.enter_context(tc.tile_pool(name="late", bufs=1))
         a_banks = [psum.tile([P, PACK, TOK], F32, name="a%d" % c, tag="bank%d" % c) for c in range(BANKS)]
@@ -202,47 +209,43 @@ def tile_list_contextual_sparse_ffn_kernel(
             for c in banks:
                 product(a_banks[c], c, a, lambda t: w1_codes[a][:, P * t : P * (t + 1)].bitcast(FP8X4), w1_planes[a][:], stop_pass[c])
 
-        per_chunk = CHUNK // TOK
-        stop_pass = [PASSES - 1 if c < per_chunk else PASSES - 2 for c in range(BANKS)]
+        starts = [sum(CHUNKS[:ci]) for ci in range(len(CHUNKS))]
+        chunk_banks = [range(m0 // TOK, (m0 + width) // TOK) for m0, width in zip(starts, CHUNKS)]
+        stop_pass = [PASSES - 1 if c in chunk_banks[0] else PASSES - 2 for c in range(BANKS)]
 
-        def close_projection(ci):
-            banks = range(ci * per_chunk, (ci + 1) * per_chunk)
-            for a in (2, 3) if ci == 0 else (3, 2):
-                project(a, banks)
+        project(0, range(BANKS))
+        project(1, range(BANKS))
+        project(2, chunk_banks[0])
+        project(3, chunk_banks[0])
 
-        h_codes, h_planes = {}, {}
+        h_bf = [late.tile([P, width * PACK], BF16, name="h_bf%d" % ci, align_bytes=64) for ci, width in enumerate(CHUNKS)]
+        h_codes = [late.tile([P, width], U32, name="h_codes%d" % ci, align_bytes=64) for ci, width in enumerate(CHUNKS)]
+        h_planes = [late.tile([P, width], U8, name="h_plane%d" % ci, align_bytes=64) for ci, width in enumerate(CHUNKS)]
 
-        def make_h(ci):
-            h_bf = late.tile([P, CHUNK * PACK], BF16, name="h_bf%d" % ci, align_bytes=64)
-            for s in range(per_chunk):
-                c = ci * per_chunk + s
-                nc.vector.tensor_tensor(
-                    h_bf[:, s * TOK * PACK : (s + 1) * TOK * PACK].rearrange("p (n t) -> p n t", t=PACK),
-                    a_banks[c][:].rearrange("p t n -> p n t"),
-                    gates[c][:],
-                    MULT,
-                )
-            h_codes[ci] = late.tile([P, CHUNK], U32, name="h_codes%d" % ci, align_bytes=64)
-            h_planes[ci] = late.tile([P, CHUNK], U8, name="h_plane%d" % ci, align_bytes=64)
-            nc.vector.quantize_mx(out=h_codes[ci][:].bitcast(FP8X4), scales=h_planes[ci][:], in_=h_bf[:])
+        def gate_product(ci, c):
+            s = c - chunk_banks[ci][0]
+            nc.vector.tensor_tensor(
+                h_bf[ci][:, s * TOK * PACK : (s + 1) * TOK * PACK].rearrange("p (n t) -> p n t", t=PACK),
+                a_banks[c][:].rearrange("p t n -> p n t"),
+                gates[c][:],
+                MULT,
+            )
 
+        def quantize_h(ci):
+            nc.vector.quantize_mx(out=h_codes[ci][:].bitcast(FP8X4), scales=h_planes[ci][:], in_=h_bf[ci][:])
+
+        units = [(ci, g) for ci in range(len(CHUNKS)) for g in range(GROUPS)]
+        ys = {(ci, g): late.tile([P, PACK, CHUNKS[ci]], F32, name="y%d_%d" % (ci, g), align_bytes=64) for ci, g in units}
+        y_codes = [late.tile([P, GROUPS, width], U32, name="y_codes%d" % ci, align_bytes=64) for ci, width in enumerate(CHUNKS)]
         y_planes = late.tile([P, GROUPS, S], U8, name="y_planes", align_bytes=64)
-        per_bank = BANK_F32 // CHUNK
-        ys = {}
-
-        def scalar_gains(ci, g):
-            if ci == 0:
-                return PACK
-            if (ci, g) == (CHUNKS - 1, GROUPS - 1):
-                return 0
-            return SCALAR_GAINS
+        fills = []
 
         def neurons(ci, g):
-            y = late.tile([P, PACK, CHUNK], F32, name="y%d_%d" % (ci, g), align_bytes=64)
-            ys[ci, g] = y
+            y, width = ys[ci, g], CHUNKS[ci]
+            per_bank = BANK_F32 // width
             for t0 in range(0, PACK, per_bank):
-                bank = (g * PACK + t0) // per_bank
-                z = psum.tile([P, per_bank, CHUNK], F32, name="z%d_%d" % (ci, bank), tag="bank%d" % bank)
+                z = psum.tile([P, per_bank, width], F32, name="z%d" % len(fills), tag="bank%d" % (len(fills) % BANKS))
+                fills.append(z)
                 for s in range(per_bank):
                     col = K_PASS * g + P * (t0 + s)
                     nc.tensor.matmul_mx(
@@ -257,41 +260,62 @@ def tile_list_contextual_sparse_ffn_kernel(
                 for s in range(per_bank):
                     t = t0 + s
                     nc.scalar.activation(y[:, t, :], z[:, s, :], ACT.Gelu_apprx_tanh, bias=bias[:, g, t : t + 1])
-            for t in range(scalar_gains(ci, g)):
+            for t in range(SCALAR_GAINS[ci]):
                 nc.scalar.activation(y[:, t, :], y[:, t, :], ACT.Copy, scale=gains[:, g, t : t + 1])
 
-        def hand_out(ci, g):
-            y = ys[ci, g]
-            m0 = ci * CHUNK
-            for t in range(scalar_gains(ci, g), PACK):
-                nc.vector.tensor_scalar(y[:, t, :], y[:, t, :], gains[:, g, t : t + 1], None, MULT)
-            nc.sync.dma_start(out_0[K_PASS * g : K_PASS * (g + 1), m0 : m0 + CHUNK].rearrange("(p t) m -> p t m", t=PACK), y[:])
-            y_bf = ring.tile([P, CHUNK * PACK], BF16, name="y_bf", align_bytes=64)
-            nc.vector.tensor_copy(
-                y_bf[:].rearrange("p (b i t) -> p b t i", t=PACK, i=PACK),
-                y[:].rearrange("p t (b i) -> p b t i", i=PACK),
-            )
-            y_codes = late.tile([P, CHUNK], U32, name="y_codes%d_%d" % (ci, g), align_bytes=64)
-            nc.vector.quantize_mx(out=y_codes[:].bitcast(FP8X4), scales=y_planes[:, g, m0 : m0 + CHUNK], in_=y_bf[:])
-            nc.sync.dma_start(
-                out_1[g].rearrange("p m t -> p (m t)")[:, PACK * m0 : PACK * (m0 + CHUNK)].bitcast(I32),
-                y_codes[:].bitcast(I32),
-            )
+        def finish_y(ci, g):
+            y, m0, width = ys[ci, g], starts[ci], CHUNKS[ci]
+            rows_out = out_0[K_PASS * g : K_PASS * (g + 1), m0 : m0 + width].rearrange("(p t) m -> p t m", t=PACK)
+            per_store = STORE_COLS // width
+            for t in range(PACK):
+                if t >= SCALAR_GAINS[ci]:
+                    nc.vector.tensor_scalar(y[:, t, :], y[:, t, :], gains[:, g, t : t + 1], None, MULT)
+                if (t + 1) % per_store == 0:
+                    nc.sync.dma_start(rows_out[:, t + 1 - per_store : t + 1, :], y[:, t + 1 - per_store : t + 1, :])
 
-        project(0, range(BANKS))
-        project(1, range(BANKS))
-        close_projection(0)
-        close_projection(1)
-        make_h(0)
-        for ci in range(CHUNKS):
-            neurons(ci, 0)
-            if ci + 1 < CHUNKS:
-                make_h(ci + 1)
-            if ci + 2 < CHUNKS:
-                close_projection(ci + 2)
-            neurons(ci, 1)
-            hand_out(ci, 0)
-            hand_out(ci, 1)
+        def round_y(ci, g, n0):
+            y_bf = ring.tile([P, PIECE * PACK], BF16, name="y_bf", align_bytes=64)
+            nc.vector.tensor_copy(
+                y_bf[:].rearrange("p (m t) -> p m t", t=PACK),
+                ys[ci, g][:, :, n0 : n0 + PIECE].rearrange("p t m -> p m t"),
+            )
+            return y_bf
+
+        def quantize_y(ci, g, n0, y_bf):
+            m0, width = starts[ci], CHUNKS[ci]
+            nc.vector.quantize_mx(
+                out=y_codes[ci][:, g, n0 : n0 + PIECE].bitcast(FP8X4), scales=y_planes[:, g, m0 + n0 : m0 + n0 + PIECE], in_=y_bf[:]
+            )
+            if n0 + PIECE == width and g == GROUPS - 1:
+                nc.sync.dma_start(
+                    out_1.rearrange("g p m t -> p g (m t)")[:, :, PACK * m0 : PACK * (m0 + width)].bitcast(I32),
+                    y_codes[ci][:].bitcast(I32),
+                )
+
+        for c in chunk_banks[0]:
+            gate_product(0, c)
+        quantize_h(0)
+        neurons(0, 0)
+        for ci in range(1, len(CHUNKS)):
+            for c in chunk_banks[ci]:
+                project(3, [c])
+                project(2, [c])
+                gate_product(ci, c)
+                if ci > 1 and c == chunk_banks[ci][0]:
+                    quantize_h(ci - 1)
+        quantize_h(len(CHUNKS) - 1)
+        finish_y(0, 0)
+        for ci, g in units[1:]:
+            neurons(ci, g)
+            finish_y(ci, g)
+        pieces = [(ci, g, n0) for ci, g in units for n0 in range(0, CHUNKS[ci], PIECE)]
+        waiting = None
+        for ci, g, n0 in pieces:
+            y_bf = round_y(ci, g, n0)
+            if waiting is not None:
+                quantize_y(*waiting)
+            waiting = (ci, g, n0, y_bf)
+        quantize_y(*waiting)
         for q in range(QUADS):
             nc.scalar.dma_start(
                 out_2[:, PACK * q : PACK * (q + 1), :].rearrange("g r m -> r g m").bitcast(I32),

@@ -29,7 +29,6 @@ BANKS = 8
 TOK = S // BANKS
 BANK_F32 = 512
 PIECE = 256
-STORE_COLS = 1024
 CHUNKS = [256, 512, 256]
 SCALAR_GAINS = [4, 1, 0]
 LAST_VECTOR = 40
@@ -142,7 +141,7 @@ def tile_list_contextual_sparse_ffn_kernel(
                     stop=(a == last and t == PACK - 1),
                 )
 
-        b_banks = [psum.tile([P, PACK, TOK], F32, name="b%d" % c, tag="bank%d" % c) for c in range(BANKS)]
+        b_banks = [psum.tile([P, HALF], F32, name="b%d" % c, tag="bank%d" % c) for c in range(BANKS)]
         half_cols = HALF // LIST_COLS
         for a in range(PASSES):
             for u in range(2):
@@ -158,8 +157,15 @@ def tile_list_contextual_sparse_ffn_kernel(
                 load_w1(2 * a - 2)
                 load_w1(2 * a - 1)
             for c in range(BANKS):
-                product(
-                    b_banks[c], c, a, lambda t: w4_codes[a][:, 2 * P * t : 2 * P * (t + 1)].bitcast(FP4X4), planes[:, a, S:], PASSES - 1
+                u, t = divmod(c, PACK)
+                nc.tensor.matmul_mx(
+                    out=b_banks[c][:],
+                    lhsT=w4_codes[a][:, 2 * P * t : 2 * P * (t + 1)].bitcast(FP4X4),
+                    lhsT_scale=planes[:, a, S + P * t : S + P * (t + 1)],
+                    rhs=v_codes[a][u][:].bitcast(FP8X4),
+                    rhs_scale=planes[:, a, u * HALF : (u + 1) * HALF],
+                    start=(a == 0),
+                    stop=(a == PASSES - 1),
                 )
 
         nc.vector.memset(v2_plane[:].bitcast(I32), 0)
@@ -171,9 +177,10 @@ def tile_list_contextual_sparse_ffn_kernel(
         nc.sync.dma_start(bias[:], bn.rearrange("(g p t) -> p g t", g=GROUPS, t=PACK))
         nc.sync.dma_start(gains[:], gain.rearrange("(g p t) -> p g t", g=GROUPS, t=PACK))
 
-        gates = [keep.tile([P, TOK, PACK], F32, name="gate%d" % c) for c in range(BANKS)]
+        gates = [keep.tile([P, PACK, HALF], F32, name="gate%d" % u) for u in range(2)]
         for c in range(BANKS):
-            nc.scalar.activation(gates[c][:], b_banks[c][:].rearrange("p t n -> p n t"), ACT.Sigmoid)
+            u, t = divmod(c, PACK)
+            nc.scalar.activation(gates[u][:, t, :], b_banks[c][:], ACT.Sigmoid)
 
         w1_codes = [keep.tile([P, H], U32, name="w1_codes%d" % a, align_bytes=64) for a in range(PASSES)]
         w1_planes = [keep.tile([P, H], U8, name="w1_plane%d" % a, align_bytes=64) for a in range(PASSES)]
@@ -191,7 +198,8 @@ def tile_list_contextual_sparse_ffn_kernel(
             else:
                 halves = [w1_last[u][:].rearrange("p j (m t) -> p m t j", t=PACK) for u in range(2)]
                 mid = P // 2
-                nc.vector.tensor_copy(dealt[:, 0:mid], halves[0])
+                nc.vector.tensor_copy(dealt[:, 0 : mid // 2], halves[0][:, 0 : mid // 2])
+                nc.scalar.copy(dealt[:, mid // 2 : mid], halves[0][:, mid // 2 :])
                 nc.vector.tensor_copy(dealt[:, mid : mid + LAST_VECTOR], halves[1][:, 0:LAST_VECTOR])
                 nc.scalar.copy(dealt[:, mid + LAST_VECTOR :], halves[1][:, LAST_VECTOR:])
                 for u in range(2):
@@ -224,10 +232,11 @@ def tile_list_contextual_sparse_ffn_kernel(
 
         def gate_product(ci, c):
             s = c - chunk_banks[ci][0]
+            u, n0 = divmod(c * TOK, HALF)
             nc.vector.tensor_tensor(
-                h_bf[ci][:, s * TOK * PACK : (s + 1) * TOK * PACK].rearrange("p (n t) -> p n t", t=PACK),
-                a_banks[c][:].rearrange("p t n -> p n t"),
-                gates[c][:],
+                h_bf[ci][:, s * TOK * PACK : (s + 1) * TOK * PACK].rearrange("p (n i t) -> p n t i", t=PACK, i=2),
+                a_banks[c][:].rearrange("p t (n i) -> p n t i", i=2),
+                gates[u][:, :, n0 : n0 + TOK].rearrange("p t (n i) -> p n t i", i=2),
                 MULT,
             )
 
@@ -260,13 +269,13 @@ def tile_list_contextual_sparse_ffn_kernel(
                 for s in range(per_bank):
                     t = t0 + s
                     nc.scalar.activation(y[:, t, :], z[:, s, :], ACT.Gelu_apprx_tanh, bias=bias[:, g, t : t + 1])
-            for t in range(SCALAR_GAINS[ci]):
-                nc.scalar.activation(y[:, t, :], y[:, t, :], ACT.Copy, scale=gains[:, g, t : t + 1])
+                for t in range(t0, min(t0 + per_bank, SCALAR_GAINS[ci])):
+                    nc.scalar.activation(y[:, t, :], y[:, t, :], ACT.Copy, scale=gains[:, g, t : t + 1])
 
         def finish_y(ci, g):
             y, m0, width = ys[ci, g], starts[ci], CHUNKS[ci]
             rows_out = out_0[K_PASS * g : K_PASS * (g + 1), m0 : m0 + width].rearrange("(p t) m -> p t m", t=PACK)
-            per_store = STORE_COLS // width
+            per_store = PACK if ci == len(CHUNKS) - 1 else 2
             for t in range(PACK):
                 if t >= SCALAR_GAINS[ci]:
                     nc.vector.tensor_scalar(y[:, t, :], y[:, t, :], gains[:, g, t : t + 1], None, MULT)

@@ -32,6 +32,7 @@ PIECE = 256
 CHUNKS = [256, 512, 256]
 SCALAR_GAINS = [4, 1, 0]
 LAST_VECTOR = 40
+PORT_ORDER = (0, 2, 1, 3)
 
 
 def tile_list_contextual_sparse_ffn_kernel(
@@ -99,8 +100,8 @@ def tile_list_contextual_sparse_ffn_kernel(
             staged[:, S:].rearrange("p (t m) -> p t m", t=PACK), w4_sc_raw[:].rearrange("p (m t) -> p t m", t=PACK)
         )
         nc.vector.tensor_copy(staged[:, 0:S].bitcast(I32), v_sc_picked[:].bitcast(I32))
-        for q in range(QUADS):
-            nc.sync.dma_start(
+        for q in PORT_ORDER:
+            nc.scalar.dma_start(
                 planes[QUAD * q : QUAD * q + PACK, :, :].bitcast(I32),
                 staged[QUAD + rows * q : QUAD + rows * (q + 1), :].bitcast(I32),
             )

@@ -29,8 +29,9 @@ BANKS = 8
 TOK = S // BANKS
 BANK_F32 = 512
 PIECE = 256
-CHUNKS = [256, 512, 256]
-SCALAR_GAINS = [4, 1, 0]
+CHUNKS = [256, 256, 512]
+SCALAR_GAINS = [4, 4, 0]
+SCALAR_PAIRS = [0, 128, 0, 64]
 LAST_VECTOR = 40
 PORT_ORDER = (0, 2, 1, 3)
 
@@ -42,7 +43,7 @@ def tile_list_contextual_sparse_ffn_kernel(
     with ExitStack() as ctx:
         lists = ctx.enter_context(tc.tile_pool(name="lists", bufs=1))
         keep = ctx.enter_context(tc.tile_pool(name="keep", bufs=1))
-        ring = ctx.enter_context(tc.tile_pool(name="ring", bufs=3))
+        ring = ctx.enter_context(tc.tile_pool(name="ring", bufs=4))
         psum = ctx.enter_context(tc.psum_pool(name="psum", bufs=1))
 
         idx = lists.tile([P, S // LIST_COLS], U16, name="idx")
@@ -227,104 +228,112 @@ def tile_list_contextual_sparse_ffn_kernel(
         project(2, chunk_banks[0])
         project(3, chunk_banks[0])
 
-        h_bf = [late.tile([P, width * PACK], BF16, name="h_bf%d" % ci, align_bytes=64) for ci, width in enumerate(CHUNKS)]
-        h_codes = [late.tile([P, width], U32, name="h_codes%d" % ci, align_bytes=64) for ci, width in enumerate(CHUNKS)]
-        h_planes = [late.tile([P, width], U8, name="h_plane%d" % ci, align_bytes=64) for ci, width in enumerate(CHUNKS)]
+        h_bf = late.tile([P, S * PACK], BF16, name="h_bf", align_bytes=64)
+        h_codes = late.tile([P, S], U32, name="h_codes", align_bytes=64)
+        h_plane = late.tile([P, S], U8, name="h_plane", align_bytes=64)
 
-        def gate_product(ci, c):
-            s = c - chunk_banks[ci][0]
+        def gate_product(c):
             u, n0 = divmod(c * TOK, HALF)
             nc.vector.tensor_tensor(
-                h_bf[ci][:, s * TOK * PACK : (s + 1) * TOK * PACK].rearrange("p (n i t) -> p n t i", t=PACK, i=2),
+                h_bf[:, c * TOK * PACK : (c + 1) * TOK * PACK].rearrange("p (n i t) -> p n t i", t=PACK, i=2),
                 a_banks[c][:].rearrange("p t (n i) -> p n t i", i=2),
                 gates[u][:, :, n0 : n0 + TOK].rearrange("p t (n i) -> p n t i", i=2),
                 MULT,
             )
 
-        def quantize_h(ci):
-            nc.vector.quantize_mx(out=h_codes[ci][:].bitcast(FP8X4), scales=h_planes[ci][:], in_=h_bf[ci][:])
+        def quantize_h(m0, width):
+            nc.vector.quantize_mx(
+                out=h_codes[:, m0 : m0 + width].bitcast(FP8X4),
+                scales=h_plane[:, m0 : m0 + width],
+                in_=h_bf[:, m0 * PACK : (m0 + width) * PACK],
+            )
 
-        units = [(ci, g) for ci in range(len(CHUNKS)) for g in range(GROUPS)]
-        ys = {(ci, g): late.tile([P, PACK, CHUNKS[ci]], F32, name="y%d_%d" % (ci, g), align_bytes=64) for ci, g in units}
-        y_codes = [late.tile([P, GROUPS, width], U32, name="y_codes%d" % ci, align_bytes=64) for ci, width in enumerate(CHUNKS)]
+        y_first = [late.tile([P, PACK, width], F32, name="y0_%d" % ci, align_bytes=64) for ci, width in enumerate(CHUNKS)]
+        y_second = late.tile([P, PACK, S], F32, name="y1", align_bytes=64)
+        y_codes = [late.tile([P, S], U32, name="y_codes%d" % g, align_bytes=64) for g in range(GROUPS)]
         y_planes = late.tile([P, GROUPS, S], U8, name="y_planes", align_bytes=64)
+        rows_out = [out_0[K_PASS * g : K_PASS * (g + 1), :].rearrange("(p t) m -> p t m", t=PACK) for g in range(GROUPS)]
         fills = []
 
-        def neurons(ci, g):
-            y, width = ys[ci, g], CHUNKS[ci]
+        def neurons(g, slots, m0, width, y, scalar_gain):
+            z = psum.tile([P, len(slots), width], F32, name="z%d" % len(fills), tag="bank%d" % (len(fills) % BANKS))
+            fills.append(z)
+            for s, t in enumerate(slots):
+                col = K_PASS * g + P * t
+                nc.tensor.matmul_mx(
+                    out=z[:, s, :],
+                    lhsT=v2_codes[:, col : col + P].bitcast(FP8X4),
+                    lhsT_scale=v2_plane[:, col : col + P],
+                    rhs=h_codes[:, m0 : m0 + width].bitcast(FP8X4),
+                    rhs_scale=h_plane[:, m0 : m0 + width],
+                    start=True,
+                    stop=True,
+                )
+            for s, t in enumerate(slots):
+                nc.scalar.activation(y(t), z[:, s, :], ACT.Gelu_apprx_tanh, bias=bias[:, g, t : t + 1])
+            if scalar_gain:
+                for t in slots:
+                    nc.scalar.activation(y(t), y(t), ACT.Copy, scale=gains[:, g, t : t + 1])
+
+        def first_group(ci):
+            m0, width, y = starts[ci], CHUNKS[ci], y_first[ci]
             per_bank = BANK_F32 // width
             for t0 in range(0, PACK, per_bank):
-                z = psum.tile([P, per_bank, width], F32, name="z%d" % len(fills), tag="bank%d" % (len(fills) % BANKS))
-                fills.append(z)
-                for s in range(per_bank):
-                    col = K_PASS * g + P * (t0 + s)
-                    nc.tensor.matmul_mx(
-                        out=z[:, s, :],
-                        lhsT=v2_codes[:, col : col + P].bitcast(FP8X4),
-                        lhsT_scale=v2_plane[:, col : col + P],
-                        rhs=h_codes[ci][:].bitcast(FP8X4),
-                        rhs_scale=h_planes[ci][:],
-                        start=True,
-                        stop=True,
-                    )
-                for s in range(per_bank):
-                    t = t0 + s
-                    nc.scalar.activation(y[:, t, :], z[:, s, :], ACT.Gelu_apprx_tanh, bias=bias[:, g, t : t + 1])
-                for t in range(t0, min(t0 + per_bank, SCALAR_GAINS[ci])):
-                    nc.scalar.activation(y[:, t, :], y[:, t, :], ACT.Copy, scale=gains[:, g, t : t + 1])
-
-        def finish_y(ci, g):
-            y, m0, width = ys[ci, g], starts[ci], CHUNKS[ci]
-            rows_out = out_0[K_PASS * g : K_PASS * (g + 1), m0 : m0 + width].rearrange("(p t) m -> p t m", t=PACK)
-            per_store = PACK if ci == len(CHUNKS) - 1 else 2
+                neurons(0, range(t0, t0 + per_bank), m0, width, lambda t: y[:, t, :], t0 < SCALAR_GAINS[ci])
             for t in range(PACK):
                 if t >= SCALAR_GAINS[ci]:
-                    nc.vector.tensor_scalar(y[:, t, :], y[:, t, :], gains[:, g, t : t + 1], None, MULT)
-                if (t + 1) % per_store == 0:
-                    nc.sync.dma_start(rows_out[:, t + 1 - per_store : t + 1, :], y[:, t + 1 - per_store : t + 1, :])
+                    nc.vector.tensor_scalar(y[:, t, :], y[:, t, :], gains[:, 0, t : t + 1], None, MULT)
+                if t % 2 == 1:
+                    nc.sync.dma_start(rows_out[0][:, t - 1 : t + 1, m0 : m0 + width], y[:, t - 1 : t + 1, :])
 
-        def round_y(ci, g, n0):
+        def second_group(t):
+            for m0 in range(0, S, HALF):
+                neurons(1, [t], m0, HALF, lambda t: y_second[:, t, m0 : m0 + HALF], False)
+                nc.vector.tensor_scalar(y_second[:, t, m0 : m0 + HALF], y_second[:, t, m0 : m0 + HALF], gains[:, 1, t : t + 1], None, MULT)
+            nc.sync.dma_start(rows_out[1][:, t, :], y_second[:, t, :])
+
+        def round_y(source, cut):
             y_bf = ring.tile([P, PIECE * PACK], BF16, name="y_bf", align_bytes=64)
-            nc.vector.tensor_copy(
-                y_bf[:].rearrange("p (m t) -> p m t", t=PACK),
-                ys[ci, g][:, :, n0 : n0 + PIECE].rearrange("p t m -> p m t"),
-            )
+            woven = y_bf[:].rearrange("p (m i t) -> p m t i", t=PACK, i=2)
+            apart = source.rearrange("p t (m i) -> p m t i", i=2)
+            if cut > 0:
+                nc.scalar.copy(woven[:, 0:cut], apart[:, 0:cut])
+            if cut < PIECE // 2:
+                nc.vector.tensor_copy(woven[:, cut:], apart[:, cut:])
             return y_bf
 
-        def quantize_y(ci, g, n0, y_bf):
-            m0, width = starts[ci], CHUNKS[ci]
+        def quantize_y(g, m0, y_bf):
             nc.vector.quantize_mx(
-                out=y_codes[ci][:, g, n0 : n0 + PIECE].bitcast(FP8X4), scales=y_planes[:, g, m0 + n0 : m0 + n0 + PIECE], in_=y_bf[:]
+                out=y_codes[g][:, m0 : m0 + PIECE].bitcast(FP8X4), scales=y_planes[:, g, m0 : m0 + PIECE], in_=y_bf[:]
             )
-            if n0 + PIECE == width and g == GROUPS - 1:
+            width = S if g == 0 else HALF
+            if (m0 + PIECE) % width == 0:
+                lo = m0 + PIECE - width
                 nc.sync.dma_start(
-                    out_1.rearrange("g p m t -> p g (m t)")[:, :, PACK * m0 : PACK * (m0 + width)].bitcast(I32),
-                    y_codes[ci][:].bitcast(I32),
+                    out_1[g].rearrange("p m t -> p (m t)")[:, PACK * lo : PACK * (lo + width)].bitcast(I32),
+                    y_codes[g][:, lo : lo + width].bitcast(I32),
                 )
 
-        for c in chunk_banks[0]:
-            gate_product(0, c)
-        quantize_h(0)
-        neurons(0, 0)
-        for ci in range(1, len(CHUNKS)):
+        for ci in range(len(CHUNKS)):
             for c in chunk_banks[ci]:
-                project(3, [c])
-                project(2, [c])
-                gate_product(ci, c)
-                if ci > 1 and c == chunk_banks[ci][0]:
-                    quantize_h(ci - 1)
-        quantize_h(len(CHUNKS) - 1)
-        finish_y(0, 0)
-        for ci, g in units[1:]:
-            neurons(ci, g)
-            finish_y(ci, g)
-        pieces = [(ci, g, n0) for ci, g in units for n0 in range(0, CHUNKS[ci], PIECE)]
+                if ci > 0:
+                    project(3, [c])
+                    project(2, [c])
+                gate_product(c)
+            quantize_h(starts[ci], CHUNKS[ci])
+            if ci > 0:
+                first_group(ci - 1)
+        first_group(len(CHUNKS) - 1)
+        for t in range(PACK):
+            second_group(t)
+        pieces = [(0, starts[ci] + n0, y_first[ci][:, :, n0 : n0 + PIECE], 0) for ci in range(len(CHUNKS)) for n0 in range(0, CHUNKS[ci], PIECE)]
+        pieces = pieces + [(1, m0, y_second[:, :, m0 : m0 + PIECE], SCALAR_PAIRS[m0 // PIECE]) for m0 in range(0, S, PIECE)]
         waiting = None
-        for ci, g, n0 in pieces:
-            y_bf = round_y(ci, g, n0)
+        for g, m0, source, cut in pieces:
+            y_bf = round_y(source, cut)
             if waiting is not None:
                 quantize_y(*waiting)
-            waiting = (ci, g, n0, y_bf)
+            waiting = (g, m0, y_bf)
         quantize_y(*waiting)
         for q in range(QUADS):
             nc.scalar.dma_start(

@@ -188,9 +188,9 @@ def tile_list_contextual_sparse_ffn_kernel(
         w1_planes = [keep.tile([P, H], U8, name="w1_plane%d" % a, align_bytes=64) for a in range(PASSES)]
         for a in range(PASSES):
             w1_bf = ring.tile([P, H * PACK], BF16, name="w1_bf", align_bytes=64)
-            dealt = w1_bf[:].rearrange("p (t m j) -> p m t j", t=PACK, j=PACK)
+            dealt = w1_bf[:].rearrange("p (t m j) -> p m j t", t=PACK, j=PACK)
             if a < PASSES - 1:
-                whole = w1_raw[a][:].rearrange("p j (m t) -> p m t j", t=PACK)
+                whole = w1_raw[a][:].rearrange("p j (m t) -> p m j t", t=PACK)
                 if a < PASSES - 2:
                     nc.vector.tensor_copy(dealt, whole)
                 else:
@@ -198,7 +198,7 @@ def tile_list_contextual_sparse_ffn_kernel(
                     nc.scalar.copy(dealt[:, 2 * LAST_VECTOR :], whole[:, 2 * LAST_VECTOR :])
                 nc.vector.quantize_mx(out=w1_codes[a][:].bitcast(FP8X4), scales=w1_planes[a][:], in_=w1_bf[:])
             else:
-                halves = [w1_last[u][:].rearrange("p j (m t) -> p m t j", t=PACK) for u in range(2)]
+                halves = [w1_last[u][:].rearrange("p j (m t) -> p m j t", t=PACK) for u in range(2)]
                 mid = P // 2
                 nc.vector.tensor_copy(dealt[:, 0 : mid // 2], halves[0][:, 0 : mid // 2])
                 nc.scalar.copy(dealt[:, mid // 2 : mid], halves[0][:, mid // 2 :])

@@ -15,6 +15,7 @@ FP8X4 = mybir.dt.float8_e4m3fn_x4
 FP4X4 = mybir.dt.float4_e2m1fn_x4
 ACT = mybir.ActivationFunctionType
 MULT = mybir.AluOpType.mult
+ADD = mybir.AluOpType.add
 
 P = 128
 PACK = 4
@@ -30,8 +31,8 @@ TOK = S // BANKS
 BANK_F32 = 512
 PIECE = 256
 CHUNKS = [256, 256, 512]
-SCALAR_GAINS = [4, 4, 0]
-SCALAR_PAIRS = [0, 128, 0, 64]
+POOL_GAINS = 0
+SCALAR_PAIRS = [0, 0, 0, 256, 32, 96]
 LAST_VECTOR = 40
 PORT_ORDER = (0, 2, 1, 3)
 
@@ -248,70 +249,59 @@ def tile_list_contextual_sparse_ffn_kernel(
                 in_=h_bf[:, m0 * PACK : (m0 + width) * PACK],
             )
 
-        y_first = [late.tile([P, PACK, width], F32, name="y0_%d" % ci, align_bytes=64) for ci, width in enumerate(CHUNKS)]
-        y_second = late.tile([P, PACK, S], F32, name="y1", align_bytes=64)
+        y = [late.tile([P, PACK, S], F32, name="y%d" % g, align_bytes=64) for g in range(GROUPS)]
         y_codes = [late.tile([P, S], U32, name="y_codes%d" % g, align_bytes=64) for g in range(GROUPS)]
         y_planes = late.tile([P, GROUPS, S], U8, name="y_planes", align_bytes=64)
         rows_out = [out_0[K_PASS * g : K_PASS * (g + 1), :].rearrange("(p t) m -> p t m", t=PACK) for g in range(GROUPS)]
         fills = []
 
-        def neurons(g, slots, m0, width, y, scalar_gain):
-            z = psum.tile([P, len(slots), width], F32, name="z%d" % len(fills), tag="bank%d" % (len(fills) % BANKS))
-            fills.append(z)
-            for s, t in enumerate(slots):
-                col = K_PASS * g + P * t
-                nc.tensor.matmul_mx(
-                    out=z[:, s, :],
-                    lhsT=v2_codes[:, col : col + P].bitcast(FP8X4),
-                    lhsT_scale=v2_plane[:, col : col + P],
-                    rhs=h_codes[:, m0 : m0 + width].bitcast(FP8X4),
-                    rhs_scale=h_plane[:, m0 : m0 + width],
-                    start=True,
-                    stop=True,
-                )
-            for s, t in enumerate(slots):
-                nc.scalar.activation(y(t), z[:, s, :], ACT.Gelu_apprx_tanh, bias=bias[:, g, t : t + 1])
-            if scalar_gain:
-                for t in slots:
-                    nc.scalar.activation(y(t), y(t), ACT.Copy, scale=gains[:, g, t : t + 1])
-
-        def first_group(ci):
-            m0, width, y = starts[ci], CHUNKS[ci], y_first[ci]
+        def neurons(g, m0, width, pool_gains):
             per_bank = BANK_F32 // width
+            cols = slice(m0, m0 + width)
             for t0 in range(0, PACK, per_bank):
-                neurons(0, range(t0, t0 + per_bank), m0, width, lambda t: y[:, t, :], t0 < SCALAR_GAINS[ci])
+                z = psum.tile([P, per_bank, width], F32, name="z%d" % len(fills), tag="bank%d" % (len(fills) % BANKS))
+                fills.append(z)
+                for s in range(per_bank):
+                    col = K_PASS * g + P * (t0 + s)
+                    nc.tensor.matmul_mx(
+                        out=z[:, s, :],
+                        lhsT=v2_codes[:, col : col + P].bitcast(FP8X4),
+                        lhsT_scale=v2_plane[:, col : col + P],
+                        rhs=h_codes[:, cols].bitcast(FP8X4),
+                        rhs_scale=h_plane[:, cols],
+                        start=True,
+                        stop=True,
+                    )
+                for s in range(per_bank):
+                    t = t0 + s
+                    nc.scalar.activation(y[g][:, t, cols], z[:, s, :], ACT.Gelu_apprx_tanh, bias=bias[:, g, t : t + 1])
             for t in range(PACK):
-                if t >= SCALAR_GAINS[ci]:
-                    nc.vector.tensor_scalar(y[:, t, :], y[:, t, :], gains[:, 0, t : t + 1], None, MULT)
+                if t < pool_gains:
+                    nc.gpsimd.tensor_scalar(y[g][:, t, cols], y[g][:, t, cols], gains[:, g, t : t + 1], 0.0, MULT, ADD)
+                else:
+                    nc.vector.tensor_scalar(y[g][:, t, cols], y[g][:, t, cols], gains[:, g, t : t + 1], None, MULT)
                 if t % 2 == 1:
-                    nc.sync.dma_start(rows_out[0][:, t - 1 : t + 1, m0 : m0 + width], y[:, t - 1 : t + 1, :])
+                    nc.sync.dma_start(rows_out[g][:, t - 1 : t + 1, cols], y[g][:, t - 1 : t + 1, cols])
 
-        def second_group(t):
-            for m0 in range(0, S, HALF):
-                neurons(1, [t], m0, HALF, lambda t: y_second[:, t, m0 : m0 + HALF], False)
-                nc.vector.tensor_scalar(y_second[:, t, m0 : m0 + HALF], y_second[:, t, m0 : m0 + HALF], gains[:, 1, t : t + 1], None, MULT)
-            nc.sync.dma_start(rows_out[1][:, t, :], y_second[:, t, :])
-
-        def round_y(source, cut):
-            y_bf = ring.tile([P, PIECE * PACK], BF16, name="y_bf", align_bytes=64)
+        def round_y(source, width, cut):
+            y_bf = ring.tile([P, width * PACK], BF16, name="y_bf", tag="w1_bf", align_bytes=64)
             woven = y_bf[:].rearrange("p (m i t) -> p m t i", t=PACK, i=2)
             apart = source.rearrange("p t (m i) -> p m t i", i=2)
             if cut > 0:
                 nc.scalar.copy(woven[:, 0:cut], apart[:, 0:cut])
-            if cut < PIECE // 2:
+            if cut < width // 2:
                 nc.vector.tensor_copy(woven[:, cut:], apart[:, cut:])
             return y_bf
 
-        def quantize_y(g, m0, y_bf):
+        def quantize_y(g, m0, width, y_bf):
             nc.vector.quantize_mx(
-                out=y_codes[g][:, m0 : m0 + PIECE].bitcast(FP8X4), scales=y_planes[:, g, m0 : m0 + PIECE], in_=y_bf[:]
+                out=y_codes[g][:, m0 : m0 + width].bitcast(FP8X4), scales=y_planes[:, g, m0 : m0 + width], in_=y_bf[:]
             )
-            width = S if g == 0 else HALF
-            if (m0 + PIECE) % width == 0:
-                lo = m0 + PIECE - width
+            if (m0 + width) % HALF == 0:
+                lo = m0 + width - HALF
                 nc.sync.dma_start(
-                    out_1[g].rearrange("p m t -> p (m t)")[:, PACK * lo : PACK * (lo + width)].bitcast(I32),
-                    y_codes[g][:, lo : lo + width].bitcast(I32),
+                    out_1[g].rearrange("p m t -> p (m t)")[:, PACK * lo : PACK * (lo + HALF)].bitcast(I32),
+                    y_codes[g][:, lo : lo + HALF].bitcast(I32),
                 )
 
         for ci in range(len(CHUNKS)):
@@ -322,18 +312,17 @@ def tile_list_contextual_sparse_ffn_kernel(
                 gate_product(c)
             quantize_h(starts[ci], CHUNKS[ci])
             if ci > 0:
-                first_group(ci - 1)
-        first_group(len(CHUNKS) - 1)
-        for t in range(PACK):
-            second_group(t)
-        pieces = [(0, starts[ci] + n0, y_first[ci][:, :, n0 : n0 + PIECE], 0) for ci in range(len(CHUNKS)) for n0 in range(0, CHUNKS[ci], PIECE)]
-        pieces = pieces + [(1, m0, y_second[:, :, m0 : m0 + PIECE], SCALAR_PAIRS[m0 // PIECE]) for m0 in range(0, S, PIECE)]
+                neurons(0, starts[ci - 1], CHUNKS[ci - 1], PACK)
+        neurons(1, 0, HALF, POOL_GAINS)
+        neurons(0, HALF, HALF, 0)
+        neurons(1, HALF, HALF, 0)
+        pieces = [(0, 0, PIECE), (0, PIECE, PIECE), (1, 0, HALF), (0, HALF, HALF), (1, HALF, PIECE), (1, HALF + PIECE, PIECE)]
         waiting = None
-        for g, m0, source, cut in pieces:
-            y_bf = round_y(source, cut)
+        for k, (g, m0, width) in enumerate(pieces):
+            y_bf = round_y(y[g][:, :, m0 : m0 + width], width, SCALAR_PAIRS[k])
             if waiting is not None:
                 quantize_y(*waiting)
-            waiting = (g, m0, y_bf)
+            waiting = (g, m0, width, y_bf)
         quantize_y(*waiting)
         for q in range(QUADS):
             nc.scalar.dma_start(

@@ -31,8 +31,8 @@ TOK = S // BANKS
 BANK_F32 = 512
 PIECE = 256
 CHUNKS = [256, 256, 512]
-POOL_GAINS = 0
-SCALAR_PAIRS = [0, 0, 0, 256, 32, 96]
+POOL_GAINS = [4, 1]
+SCALAR_PAIRS = [0, 0, 0, 256, 64, 112]
 LAST_VECTOR = 40
 PORT_ORDER = (0, 2, 1, 3)
 
@@ -131,9 +131,9 @@ def tile_list_contextual_sparse_ffn_kernel(
             [keep.tile([P, HALF], U32, name="v_codes%d_%d" % (a, u), align_bytes=64) for u in range(2)] for a in range(PASSES)
         ]
 
-        def product(bank, c, a, codes, w_plane, last):
+        def product(bank, c, a, codes, w_plane, last, slots=range(PACK)):
             u, n0 = divmod(c * TOK, HALF)
-            for t in range(PACK):
+            for t in slots:
                 nc.tensor.matmul_mx(
                     out=bank[:, t, :],
                     lhsT=codes(t),
@@ -227,7 +227,9 @@ def tile_list_contextual_sparse_ffn_kernel(
         project(0, range(BANKS))
         project(1, range(BANKS))
         project(2, chunk_banks[0])
-        project(3, chunk_banks[0])
+        for slots in (range(0, 2), range(2, PACK)):
+            for c in chunk_banks[0]:
+                product(a_banks[c], c, 3, lambda t: w1_codes[3][:, P * t : P * (t + 1)].bitcast(FP8X4), w1_planes[3][:], stop_pass[c], slots)
 
         h_bf = late.tile([P, S * PACK], BF16, name="h_bf", align_bytes=64)
         h_codes = late.tile([P, S], U32, name="h_codes", align_bytes=64)
@@ -297,11 +299,12 @@ def tile_list_contextual_sparse_ffn_kernel(
             nc.vector.quantize_mx(
                 out=y_codes[g][:, m0 : m0 + width].bitcast(FP8X4), scales=y_planes[:, g, m0 : m0 + width], in_=y_bf[:]
             )
-            if (m0 + width) % HALF == 0:
-                lo = m0 + width - HALF
+            span = PIECE if (g, m0 // HALF) == (1, 1) else HALF
+            if (m0 + width) % span == 0:
+                lo = m0 + width - span
                 nc.sync.dma_start(
-                    out_1[g].rearrange("p m t -> p (m t)")[:, PACK * lo : PACK * (lo + HALF)].bitcast(I32),
-                    y_codes[g][:, lo : lo + HALF].bitcast(I32),
+                    out_1[g].rearrange("p m t -> p (m t)")[:, PACK * lo : PACK * (lo + span)].bitcast(I32),
+                    y_codes[g][:, lo : lo + span].bitcast(I32),
                 )
 
         for ci in range(len(CHUNKS)):
@@ -312,8 +315,8 @@ def tile_list_contextual_sparse_ffn_kernel(
                 gate_product(c)
             quantize_h(starts[ci], CHUNKS[ci])
             if ci > 0:
-                neurons(0, starts[ci - 1], CHUNKS[ci - 1], PACK)
-        neurons(1, 0, HALF, POOL_GAINS)
+                neurons(0, starts[ci - 1], CHUNKS[ci - 1], POOL_GAINS[ci - 1])
+        neurons(1, 0, HALF, 0)
         neurons(0, HALF, HALF, 0)
         neurons(1, HALF, HALF, 0)
         pieces = [(0, 0, PIECE), (0, PIECE, PIECE), (1, 0, HALF), (0, HALF, HALF), (1, HALF, PIECE), (1, HALF + PIECE, PIECE)]

@@ -32,8 +32,10 @@ BANK_F32 = 512
 PIECE = 256
 CHUNKS = [256, 256, 512]
 POOL_GAINS = [4, 1]
-SCALAR_PAIRS = [0, 0, 0, 256, 64, 112]
+SCALAR_GAINS = [0, 0]
+SCALAR_PAIRS = [256, 64, 112]
 LAST_VECTOR = 40
+FREED_EARLY = 5
 PORT_ORDER = (0, 2, 1, 3)
 
 
@@ -140,7 +142,7 @@ def tile_list_contextual_sparse_ffn_kernel(
                     lhsT_scale=w_plane[:, P * t : P * (t + 1)],
                     rhs=v_codes[a][u][:, n0 : n0 + TOK].bitcast(FP8X4),
                     rhs_scale=planes[:, a, c * TOK : (c + 1) * TOK],
-                    start=(a == 0 and t == 0),
+                    start=(a == (0 if c < FREED_EARLY else 1) and t == 0),
                     stop=(a == last and t == PACK - 1),
                 )
 
@@ -193,11 +195,11 @@ def tile_list_contextual_sparse_ffn_kernel(
             if a < PASSES - 1:
                 whole = w1_raw[a][:].rearrange("p j (m t) -> p m j t", t=PACK)
                 if a < PASSES - 2:
-                    nc.vector.tensor_copy(dealt, whole)
+                    for u in range(2):
+                        nc.vector.tensor_copy(dealt[:, :, :, 2 * u : 2 * u + 2], whole[:, :, :, 2 * u : 2 * u + 2])
                 else:
                     nc.vector.tensor_copy(dealt[:, 0 : 2 * LAST_VECTOR], whole[:, 0 : 2 * LAST_VECTOR])
                     nc.scalar.copy(dealt[:, 2 * LAST_VECTOR :], whole[:, 2 * LAST_VECTOR :])
-                nc.vector.quantize_mx(out=w1_codes[a][:].bitcast(FP8X4), scales=w1_planes[a][:], in_=w1_bf[:])
             else:
                 halves = [w1_last[u][:].rearrange("p j (m t) -> p m j t", t=PACK) for u in range(2)]
                 mid = P // 2
@@ -205,27 +207,32 @@ def tile_list_contextual_sparse_ffn_kernel(
                 nc.scalar.copy(dealt[:, mid // 2 : mid], halves[0][:, mid // 2 :])
                 nc.vector.tensor_copy(dealt[:, mid : mid + LAST_VECTOR], halves[1][:, 0:LAST_VECTOR])
                 nc.scalar.copy(dealt[:, mid + LAST_VECTOR :], halves[1][:, LAST_VECTOR:])
-                for u in range(2):
-                    cols = slice(u * H // 2, (u + 1) * H // 2)
-                    nc.vector.quantize_mx(
-                        out=w1_codes[a][:, cols].bitcast(FP8X4),
-                        scales=w1_planes[a][:, cols],
-                        in_=w1_bf[:, u * H * PACK // 2 : (u + 1) * H * PACK // 2],
-                    )
+            steps = 1 if a == PASSES - 2 else 2
+            for u in range(steps):
+                cols = slice(u * H // steps, (u + 1) * H // steps)
+                nc.vector.quantize_mx(
+                    out=w1_codes[a][:, cols].bitcast(FP8X4),
+                    scales=w1_planes[a][:, cols],
+                    in_=w1_bf[:, u * H * PACK // steps : (u + 1) * H * PACK // steps],
+                )
 
         late = ctx.enter_context(tc.tile_pool(name="late", bufs=1))
         a_banks = [psum.tile([P, PACK, TOK], F32, name="a%d" % c, tag="bank%d" % c) for c in range(BANKS)]
 
-        def project(a, banks):
+        def project(a, banks, slots=range(PACK)):
             for c in banks:
-                product(a_banks[c], c, a, lambda t: w1_codes[a][:, P * t : P * (t + 1)].bitcast(FP8X4), w1_planes[a][:], stop_pass[c])
+                product(a_banks[c], c, a, lambda t: w1_codes[a][:, P * t : P * (t + 1)].bitcast(FP8X4), w1_planes[a][:], stop_pass[c], slots)
 
         starts = [sum(CHUNKS[:ci]) for ci in range(len(CHUNKS))]
         chunk_banks = [range(m0 // TOK, (m0 + width) // TOK) for m0, width in zip(starts, CHUNKS)]
         stop_pass = [PASSES - 1 if c in chunk_banks[0] else PASSES - 2 for c in range(BANKS)]
 
-        project(0, range(BANKS))
-        project(1, range(BANKS))
+        for banks in (range(0, 2), range(2, FREED_EARLY)):
+            project(0, banks, range(0, 2))
+            project(0, banks, range(2, PACK))
+        project(1, range(BANKS), range(0, 2))
+        project(1, range(BANKS), range(2, PACK))
+        project(0, range(FREED_EARLY, BANKS - 1))
         project(2, chunk_banks[0])
         for slots in (range(0, 2), range(2, PACK)):
             for c in chunk_banks[0]:
@@ -257,11 +264,11 @@ def tile_list_contextual_sparse_ffn_kernel(
         rows_out = [out_0[K_PASS * g : K_PASS * (g + 1), :].rearrange("(p t) m -> p t m", t=PACK) for g in range(GROUPS)]
         fills = []
 
-        def neurons(g, m0, width, pool_gains):
+        def neurons(g, m0, width, scalar_gains=0):
             per_bank = BANK_F32 // width
             cols = slice(m0, m0 + width)
             for t0 in range(0, PACK, per_bank):
-                z = psum.tile([P, per_bank, width], F32, name="z%d" % len(fills), tag="bank%d" % (len(fills) % BANKS))
+                z = psum.tile([P, per_bank, width], F32, name="z%d" % len(fills), tag="bank%d" % (len(fills) % PACK + (PACK if len(fills) // PACK == 2 else 0)))
                 fills.append(z)
                 for s in range(per_bank):
                     col = K_PASS * g + P * (t0 + s)
@@ -277,10 +284,16 @@ def tile_list_contextual_sparse_ffn_kernel(
                 for s in range(per_bank):
                     t = t0 + s
                     nc.scalar.activation(y[g][:, t, cols], z[:, s, :], ACT.Gelu_apprx_tanh, bias=bias[:, g, t : t + 1])
+                for t in range(t0, t0 + per_bank):
+                    if t >= PACK - scalar_gains:
+                        nc.scalar.activation(y[g][:, t, cols], y[g][:, t, cols], ACT.Copy, scale=gains[:, g, t : t + 1])
+
+        def scale(g, m0, width, pool_gains=0, scalar_gains=0):
+            cols = slice(m0, m0 + width)
             for t in range(PACK):
                 if t < pool_gains:
                     nc.gpsimd.tensor_scalar(y[g][:, t, cols], y[g][:, t, cols], gains[:, g, t : t + 1], 0.0, MULT, ADD)
-                else:
+                elif t < PACK - scalar_gains:
                     nc.vector.tensor_scalar(y[g][:, t, cols], y[g][:, t, cols], gains[:, g, t : t + 1], None, MULT)
                 if t % 2 == 1:
                     nc.sync.dma_start(rows_out[g][:, t - 1 : t + 1, cols], y[g][:, t - 1 : t + 1, cols])
@@ -307,26 +320,50 @@ def tile_list_contextual_sparse_ffn_kernel(
                     y_codes[g][:, lo : lo + span].bitcast(I32),
                 )
 
-        for ci in range(len(CHUNKS)):
+        def finish(banks):
+            for c in banks:
+                project(3, [c])
+                if c == BANKS - 1:
+                    project(0, [c])
+                project(2, [c])
+
+        def hidden(ci):
             for c in chunk_banks[ci]:
-                if ci > 0:
-                    project(3, [c])
-                    project(2, [c])
                 gate_product(c)
             quantize_h(starts[ci], CHUNKS[ci])
-            if ci > 0:
-                neurons(0, starts[ci - 1], CHUNKS[ci - 1], POOL_GAINS[ci - 1])
-        neurons(1, 0, HALF, 0)
-        neurons(0, HALF, HALF, 0)
-        neurons(1, HALF, HALF, 0)
-        pieces = [(0, 0, PIECE), (0, PIECE, PIECE), (1, 0, HALF), (0, HALF, HALF), (1, HALF, PIECE), (1, HALF + PIECE, PIECE)]
-        waiting = None
-        for k, (g, m0, width) in enumerate(pieces):
-            y_bf = round_y(y[g][:, :, m0 : m0 + width], width, SCALAR_PAIRS[k])
-            if waiting is not None:
-                quantize_y(*waiting)
-            waiting = (g, m0, width, y_bf)
-        quantize_y(*waiting)
+
+        hidden(0)
+        finish(chunk_banks[1])
+        hidden(1)
+        finish(range(4, 5))
+        neurons(0, starts[0], CHUNKS[0])
+        finish(range(5, 7))
+        neurons(0, starts[1], CHUNKS[1])
+        finish(range(7, BANKS))
+        scale(0, starts[0], CHUNKS[0], POOL_GAINS[0])
+        hidden(2)
+        scale(0, starts[1], CHUNKS[1], POOL_GAINS[1])
+        waiting = []
+
+        def planes_of(g, m0, width, cut=0):
+            y_bf = round_y(y[g][:, :, m0 : m0 + width], width, cut)
+            if waiting:
+                quantize_y(*waiting.pop())
+            waiting.append((g, m0, width, y_bf))
+
+        neurons(1, 0, HALF)
+        neurons(0, HALF, HALF)
+        neurons(1, HALF, HALF)
+        scale(1, 0, HALF)
+        scale(0, HALF, HALF)
+        scale(1, HALF, HALF)
+        planes_of(0, 0, PIECE)
+        planes_of(0, PIECE, PIECE)
+        planes_of(1, 0, HALF)
+        planes_of(0, HALF, HALF, SCALAR_PAIRS[0])
+        planes_of(1, HALF, PIECE, SCALAR_PAIRS[1])
+        planes_of(1, HALF + PIECE, PIECE, SCALAR_PAIRS[2])
+        quantize_y(*waiting.pop())
         for q in range(QUADS):
             nc.scalar.dma_start(
                 out_2[:, PACK * q : PACK * (q + 1), :].rearrange("g r m -> r g m").bitcast(I32),

@@ -23,20 +23,22 @@ K_PASS = P * PACK
 PASSES = K // K_PASS
 GROUPS = S2 // K_PASS
 QUADS = 4
-QUAD = 32
-LIST_COLS = 16
-HALF = S // 2
+QUAD = P // QUADS
+LIST_ROWS = 16
 BANKS = 8
-TOK = S // BANKS
 BANK_F32 = 512
-PIECE = 256
-CHUNKS = [256, 256, 512]
+HALF = S // 2
+TOK = S // BANKS
+QUARTER = S // 4
+FIRST_PAIR, SECOND_PAIR = range(0, 2), range(2, PACK)
+
+CHUNKS = [QUARTER, QUARTER, HALF]
 POOL_GAINS = [4, 1]
-SCALAR_GAINS = [0, 0]
-SCALAR_PAIRS = [256, 64, 112]
-LAST_VECTOR = 40
+SCALAR_PAIRS = [256, 96, 112]
+THIRD_VECTOR = 96
 FREED_EARLY = 5
-PORT_ORDER = (0, 2, 1, 3)
+BEFORE_NEURONS = [5, 7]
+WOVEN_BUFS = 4
 
 
 def tile_list_contextual_sparse_ffn_kernel(
@@ -46,29 +48,29 @@ def tile_list_contextual_sparse_ffn_kernel(
     with ExitStack() as ctx:
         lists = ctx.enter_context(tc.tile_pool(name="lists", bufs=1))
         keep = ctx.enter_context(tc.tile_pool(name="keep", bufs=1))
-        ring = ctx.enter_context(tc.tile_pool(name="ring", bufs=4))
+        ring = ctx.enter_context(tc.tile_pool(name="ring", bufs=WOVEN_BUFS))
         psum = ctx.enter_context(tc.psum_pool(name="psum", bufs=1))
 
-        idx = lists.tile([P, S // LIST_COLS], U16, name="idx")
-        idx2 = lists.tile([P, S2 // LIST_COLS], U16, name="idx2")
+        idx = lists.tile([P, S // LIST_ROWS], U16, name="idx")
+        idx2 = lists.tile([P, S2 // LIST_ROWS], U16, name="idx2")
 
-        tables = ctx.enter_context(tc.tile_pool(name="tables", bufs=1))
+        shared = ctx.enter_context(tc.tile_pool(name="shared", bufs=1))
         region = T * 4
-        tab_sc = tables.tile([P, T], U8, name="tab_sc", offset=region)
-        w4_raw = tables.tile([P, PASSES, 2 * H], U8, name="w4_raw", offset=2 * region)
-        tab_w = [tables.tile([P, T], U32, name="tab_w%d" % a, offset=(a % 3) * region) for a in range(PASSES)]
-        w1_raw = [tables.tile([P, PACK, H], F32, name="w1_raw%d" % a, offset=region + a * region // 2) for a in range(PASSES - 1)]
+        tab_sc = shared.tile([P, T], U8, name="tab_sc", offset=region)
+        w4_raw = shared.tile([P, PASSES, 2 * H], U8, name="w4_raw", offset=2 * region)
+        tab_w = [shared.tile([P, T], U32, name="tab_w%d" % a, offset=(a % 3) * region) for a in range(PASSES)]
+        w1_raw = [shared.tile([P, PACK, H], F32, name="w1_raw%d" % a, offset=region + a * region // 2) for a in range(PASSES - 1)]
         w1_last = [
-            tables.tile([P, PACK, H // 2], F32, name="w1_last%d" % u, offset=region + (2 * (PASSES - 1) + u) * region // 4)
+            shared.tile([P, PACK, H // 2], F32, name="w1_last%d" % u, offset=region + (2 * (PASSES - 1) + u) * region // 4)
             for u in range(2)
         ]
         w4_sc_raw = keep.tile([P, H], U8, name="w4_sc_raw", align_bytes=64)
         tab2_sc = keep.tile([P, T2], U8, name="tab2_sc", align_bytes=64)
         tab2_w = keep.tile([P, T2], U32, name="tab2_w", align_bytes=64)
         planes = keep.tile([P, PASSES, S + H], U8, name="planes", align_bytes=64)
-        v2_plane = tables.tile([P, S2], U8, name="v2_plane", offset=0, align_bytes=64)
-        bias = tables.tile([P, GROUPS, PACK], F32, name="bias", offset=S2)
-        gains = tables.tile([P, GROUPS, PACK], F32, name="gains", offset=S2 + 64)
+        v2_plane = shared.tile([P, S2], U8, name="v2_plane", offset=0, align_bytes=64)
+        bias = shared.tile([P, GROUPS, PACK], F32, name="bias", offset=S2)
+        gains = shared.tile([P, GROUPS, PACK], F32, name="gains", offset=S2 + 64)
         rows = PACK * PASSES
 
         def load_table(a):
@@ -97,14 +99,14 @@ def tile_list_contextual_sparse_ffn_kernel(
         nc.vector.memset(tab2_sc[0 : P - rows, :].bitcast(I32), 0)
         nc.vector.memset(planes[:].bitcast(I32), 0)
 
-        v_sc_picked = tables.tile([P, S], U8, name="v_sc_picked", offset=region + T)
+        v_sc_picked = shared.tile([P, S], U8, name="v_sc_picked", offset=region + T)
         staged = keep.tile([P, S + H], U8, name="staged", align_bytes=64)
         nc.vector.tensor_copy(v_sc_picked[:], tab_sc[:].indirect(idx[:]))
         nc.vector.tensor_copy(
             staged[:, S:].rearrange("p (t m) -> p t m", t=PACK), w4_sc_raw[:].rearrange("p (m t) -> p t m", t=PACK)
         )
         nc.vector.tensor_copy(staged[:, 0:S].bitcast(I32), v_sc_picked[:].bitcast(I32))
-        for q in PORT_ORDER:
+        for q in (0, 2, 1, 3):
             nc.scalar.dma_start(
                 planes[QUAD * q : QUAD * q + PACK, :, :].bitcast(I32),
                 staged[QUAD + rows * q : QUAD + rows * (q + 1), :].bitcast(I32),
@@ -132,27 +134,13 @@ def tile_list_contextual_sparse_ffn_kernel(
         v_codes = [
             [keep.tile([P, HALF], U32, name="v_codes%d_%d" % (a, u), align_bytes=64) for u in range(2)] for a in range(PASSES)
         ]
-
-        def product(bank, c, a, codes, w_plane, last, slots=range(PACK)):
-            u, n0 = divmod(c * TOK, HALF)
-            for t in slots:
-                nc.tensor.matmul_mx(
-                    out=bank[:, t, :],
-                    lhsT=codes(t),
-                    lhsT_scale=w_plane[:, P * t : P * (t + 1)],
-                    rhs=v_codes[a][u][:, n0 : n0 + TOK].bitcast(FP8X4),
-                    rhs_scale=planes[:, a, c * TOK : (c + 1) * TOK],
-                    start=(a == (0 if c < FREED_EARLY else 1) and t == 0),
-                    stop=(a == last and t == PACK - 1),
-                )
-
         b_banks = [psum.tile([P, HALF], F32, name="b%d" % c, tag="bank%d" % c) for c in range(BANKS)]
-        half_cols = HALF // LIST_COLS
+        half_cols = HALF // LIST_ROWS
         for a in range(PASSES):
             for u in range(2):
                 nc.vector.tensor_copy(v_codes[a][u][:], tab_w[a][:].indirect(idx[:, u * half_cols : (u + 1) * half_cols]))
             if a == 0:
-                load_table(3)
+                load_table(PASSES - 1)
                 nc.vector.tensor_copy(v2_picked[:], tab2_w[:].indirect(idx2[:]))
                 nc.vector.tensor_copy(
                     v2_codes[:].bitcast(I32).rearrange("p (g t b i) -> p g b t i", g=GROUPS, t=PACK, i=PACK),
@@ -190,68 +178,83 @@ def tile_list_contextual_sparse_ffn_kernel(
         w1_codes = [keep.tile([P, H], U32, name="w1_codes%d" % a, align_bytes=64) for a in range(PASSES)]
         w1_planes = [keep.tile([P, H], U8, name="w1_plane%d" % a, align_bytes=64) for a in range(PASSES)]
         for a in range(PASSES):
-            w1_bf = ring.tile([P, H * PACK], BF16, name="w1_bf", align_bytes=64)
+            w1_bf = ring.tile([P, H * PACK], BF16, name="woven", align_bytes=64)
             dealt = w1_bf[:].rearrange("p (t m j) -> p m j t", t=PACK, j=PACK)
-            if a < PASSES - 1:
+            if a < PASSES - 2:
                 whole = w1_raw[a][:].rearrange("p j (m t) -> p m j t", t=PACK)
-                if a < PASSES - 2:
-                    for u in range(2):
-                        nc.vector.tensor_copy(dealt[:, :, :, 2 * u : 2 * u + 2], whole[:, :, :, 2 * u : 2 * u + 2])
-                else:
-                    nc.vector.tensor_copy(dealt[:, 0 : 2 * LAST_VECTOR], whole[:, 0 : 2 * LAST_VECTOR])
-                    nc.scalar.copy(dealt[:, 2 * LAST_VECTOR :], whole[:, 2 * LAST_VECTOR :])
+                for u in range(2):
+                    nc.vector.tensor_copy(dealt[:, :, :, 2 * u : 2 * u + 2], whole[:, :, :, 2 * u : 2 * u + 2])
+            elif a == PASSES - 2:
+                whole = w1_raw[a][:].rearrange("p j (m t) -> p m j t", t=PACK)
+                nc.vector.tensor_copy(dealt[:, 0:THIRD_VECTOR], whole[:, 0:THIRD_VECTOR])
+                nc.scalar.copy(dealt[:, THIRD_VECTOR:], whole[:, THIRD_VECTOR:])
             else:
-                halves = [w1_last[u][:].rearrange("p j (m t) -> p m j t", t=PACK) for u in range(2)]
-                mid = P // 2
-                nc.vector.tensor_copy(dealt[:, 0 : mid // 2], halves[0][:, 0 : mid // 2])
-                nc.scalar.copy(dealt[:, mid // 2 : mid], halves[0][:, mid // 2 :])
-                nc.vector.tensor_copy(dealt[:, mid : mid + LAST_VECTOR], halves[1][:, 0:LAST_VECTOR])
-                nc.scalar.copy(dealt[:, mid + LAST_VECTOR :], halves[1][:, LAST_VECTOR:])
-            steps = 1 if a == PASSES - 2 else 2
-            for u in range(steps):
-                cols = slice(u * H // steps, (u + 1) * H // steps)
+                for u in range(2):
+                    half = w1_last[u][:].rearrange("p j (m t) -> p m j t", t=PACK)
+                    places = slice(u * P // 2, (u + 1) * P // 2)
+                    nc.vector.tensor_copy(dealt[:, places, :, 0:2], half[:, :, :, 0:2])
+                    nc.scalar.copy(dealt[:, places, :, 2:PACK], half[:, :, :, 2:PACK])
+            calls = 1 if a == PASSES - 2 else 2
+            for u in range(calls):
+                cols = slice(u * H // calls, (u + 1) * H // calls)
                 nc.vector.quantize_mx(
                     out=w1_codes[a][:, cols].bitcast(FP8X4),
                     scales=w1_planes[a][:, cols],
-                    in_=w1_bf[:, u * H * PACK // steps : (u + 1) * H * PACK // steps],
+                    in_=w1_bf[:, u * H * PACK // calls : (u + 1) * H * PACK // calls],
                 )
 
         late = ctx.enter_context(tc.tile_pool(name="late", bufs=1))
         a_banks = [psum.tile([P, PACK, TOK], F32, name="a%d" % c, tag="bank%d" % c) for c in range(BANKS)]
+        starts = [sum(CHUNKS[:ci]) for ci in range(len(CHUNKS))]
+        chunk_banks = [range(m0 // TOK, (m0 + width) // TOK) for m0, width in zip(starts, CHUNKS)]
 
         def project(a, banks, slots=range(PACK)):
             for c in banks:
-                product(a_banks[c], c, a, lambda t: w1_codes[a][:, P * t : P * (t + 1)].bitcast(FP8X4), w1_planes[a][:], stop_pass[c], slots)
+                u, n0 = divmod(c * TOK, HALF)
+                first_pass = 0 if c < FREED_EARLY else 1
+                last_pass = 3 if c in chunk_banks[0] else 2
+                for t in slots:
+                    nc.tensor.matmul_mx(
+                        out=a_banks[c][:, t, :],
+                        lhsT=w1_codes[a][:, P * t : P * (t + 1)].bitcast(FP8X4),
+                        lhsT_scale=w1_planes[a][:, P * t : P * (t + 1)],
+                        rhs=v_codes[a][u][:, n0 : n0 + TOK].bitcast(FP8X4),
+                        rhs_scale=planes[:, a, c * TOK : (c + 1) * TOK],
+                        start=(a == first_pass and t == 0),
+                        stop=(a == last_pass and t == PACK - 1),
+                    )
 
-        starts = [sum(CHUNKS[:ci]) for ci in range(len(CHUNKS))]
-        chunk_banks = [range(m0 // TOK, (m0 + width) // TOK) for m0, width in zip(starts, CHUNKS)]
-        stop_pass = [PASSES - 1 if c in chunk_banks[0] else PASSES - 2 for c in range(BANKS)]
-
-        for banks in (range(0, 2), range(2, FREED_EARLY)):
-            project(0, banks, range(0, 2))
-            project(0, banks, range(2, PACK))
-        project(1, range(BANKS), range(0, 2))
-        project(1, range(BANKS), range(2, PACK))
+        for banks in (chunk_banks[0], range(len(chunk_banks[0]), FREED_EARLY)):
+            project(0, banks, FIRST_PAIR)
+            project(0, banks, SECOND_PAIR)
+        project(1, range(BANKS), FIRST_PAIR)
+        project(1, range(BANKS), SECOND_PAIR)
         project(0, range(FREED_EARLY, BANKS - 1))
         project(2, chunk_banks[0])
-        for slots in (range(0, 2), range(2, PACK)):
-            for c in chunk_banks[0]:
-                product(a_banks[c], c, 3, lambda t: w1_codes[3][:, P * t : P * (t + 1)].bitcast(FP8X4), w1_planes[3][:], stop_pass[c], slots)
+        project(3, chunk_banks[0], FIRST_PAIR)
+        project(3, chunk_banks[0], SECOND_PAIR)
+
+        def finish(banks):
+            for c in banks:
+                project(3, [c])
+                if c == BANKS - 1:
+                    project(0, [c])
+                project(2, [c])
 
         h_bf = late.tile([P, S * PACK], BF16, name="h_bf", align_bytes=64)
         h_codes = late.tile([P, S], U32, name="h_codes", align_bytes=64)
         h_plane = late.tile([P, S], U8, name="h_plane", align_bytes=64)
 
-        def gate_product(c):
-            u, n0 = divmod(c * TOK, HALF)
-            nc.vector.tensor_tensor(
-                h_bf[:, c * TOK * PACK : (c + 1) * TOK * PACK].rearrange("p (n i t) -> p n t i", t=PACK, i=2),
-                a_banks[c][:].rearrange("p t (n i) -> p n t i", i=2),
-                gates[u][:, :, n0 : n0 + TOK].rearrange("p t (n i) -> p n t i", i=2),
-                MULT,
-            )
-
-        def quantize_h(m0, width):
+        def hidden(ci):
+            for c in chunk_banks[ci]:
+                u, n0 = divmod(c * TOK, HALF)
+                nc.vector.tensor_tensor(
+                    h_bf[:, c * TOK * PACK : (c + 1) * TOK * PACK].rearrange("p (n i t) -> p n t i", t=PACK, i=2),
+                    a_banks[c][:].rearrange("p t (n i) -> p n t i", i=2),
+                    gates[u][:, :, n0 : n0 + TOK].rearrange("p t (n i) -> p n t i", i=2),
+                    MULT,
+                )
+            m0, width = starts[ci], CHUNKS[ci]
             nc.vector.quantize_mx(
                 out=h_codes[:, m0 : m0 + width].bitcast(FP8X4),
                 scales=h_plane[:, m0 : m0 + width],
@@ -262,14 +265,12 @@ def tile_list_contextual_sparse_ffn_kernel(
         y_codes = [late.tile([P, S], U32, name="y_codes%d" % g, align_bytes=64) for g in range(GROUPS)]
         y_planes = late.tile([P, GROUPS, S], U8, name="y_planes", align_bytes=64)
         rows_out = [out_0[K_PASS * g : K_PASS * (g + 1), :].rearrange("(p t) m -> p t m", t=PACK) for g in range(GROUPS)]
-        fills = []
 
-        def neurons(g, m0, width, scalar_gains=0):
+        def neurons(g, m0, width, bank0):
             per_bank = BANK_F32 // width
             cols = slice(m0, m0 + width)
             for t0 in range(0, PACK, per_bank):
-                z = psum.tile([P, per_bank, width], F32, name="z%d" % len(fills), tag="bank%d" % (len(fills) % PACK + (PACK if len(fills) // PACK == 2 else 0)))
-                fills.append(z)
+                z = psum.tile([P, per_bank, width], F32, name="z%d_%d_%d" % (g, m0, t0), tag="bank%d" % (bank0 + t0 // per_bank))
                 for s in range(per_bank):
                     col = K_PASS * g + P * (t0 + s)
                     nc.tensor.matmul_mx(
@@ -284,35 +285,31 @@ def tile_list_contextual_sparse_ffn_kernel(
                 for s in range(per_bank):
                     t = t0 + s
                     nc.scalar.activation(y[g][:, t, cols], z[:, s, :], ACT.Gelu_apprx_tanh, bias=bias[:, g, t : t + 1])
-                for t in range(t0, t0 + per_bank):
-                    if t >= PACK - scalar_gains:
-                        nc.scalar.activation(y[g][:, t, cols], y[g][:, t, cols], ACT.Copy, scale=gains[:, g, t : t + 1])
 
-        def scale(g, m0, width, pool_gains=0, scalar_gains=0):
+        def scale(g, m0, width, pool_gains=0):
             cols = slice(m0, m0 + width)
             for t in range(PACK):
                 if t < pool_gains:
                     nc.gpsimd.tensor_scalar(y[g][:, t, cols], y[g][:, t, cols], gains[:, g, t : t + 1], 0.0, MULT, ADD)
-                elif t < PACK - scalar_gains:
+                else:
                     nc.vector.tensor_scalar(y[g][:, t, cols], y[g][:, t, cols], gains[:, g, t : t + 1], None, MULT)
                 if t % 2 == 1:
                     nc.sync.dma_start(rows_out[g][:, t - 1 : t + 1, cols], y[g][:, t - 1 : t + 1, cols])
 
-        def round_y(source, width, cut):
-            y_bf = ring.tile([P, width * PACK], BF16, name="y_bf", tag="w1_bf", align_bytes=64)
-            woven = y_bf[:].rearrange("p (m i t) -> p m t i", t=PACK, i=2)
-            apart = source.rearrange("p t (m i) -> p m t i", i=2)
-            if cut > 0:
-                nc.scalar.copy(woven[:, 0:cut], apart[:, 0:cut])
-            if cut < width // 2:
-                nc.vector.tensor_copy(woven[:, cut:], apart[:, cut:])
+        def round_y(g, m0, width, scalar_pairs):
+            y_bf = ring.tile([P, width * PACK], BF16, name="woven", align_bytes=64)
+            woven = y_bf[:].rearrange("p (n i t) -> p n t i", t=PACK, i=2)
+            apart = y[g][:, :, m0 : m0 + width].rearrange("p t (n i) -> p n t i", i=2)
+            if scalar_pairs > 0:
+                nc.scalar.copy(woven[:, 0:scalar_pairs], apart[:, 0:scalar_pairs])
+            if scalar_pairs < width // 2:
+                nc.vector.tensor_copy(woven[:, scalar_pairs:], apart[:, scalar_pairs:])
             return y_bf
 
-        def quantize_y(g, m0, width, y_bf):
+        def quantize_y(g, m0, width, span, y_bf):
             nc.vector.quantize_mx(
                 out=y_codes[g][:, m0 : m0 + width].bitcast(FP8X4), scales=y_planes[:, g, m0 : m0 + width], in_=y_bf[:]
             )
-            span = PIECE if (g, m0 // HALF) == (1, 1) else HALF
             if (m0 + width) % span == 0:
                 lo = m0 + width - span
                 nc.sync.dma_start(
@@ -320,50 +317,39 @@ def tile_list_contextual_sparse_ffn_kernel(
                     y_codes[g][:, lo : lo + span].bitcast(I32),
                 )
 
-        def finish(banks):
-            for c in banks:
-                project(3, [c])
-                if c == BANKS - 1:
-                    project(0, [c])
-                project(2, [c])
-
-        def hidden(ci):
-            for c in chunk_banks[ci]:
-                gate_product(c)
-            quantize_h(starts[ci], CHUNKS[ci])
-
         hidden(0)
         finish(chunk_banks[1])
         hidden(1)
-        finish(range(4, 5))
-        neurons(0, starts[0], CHUNKS[0])
-        finish(range(5, 7))
-        neurons(0, starts[1], CHUNKS[1])
-        finish(range(7, BANKS))
+        finish(range(chunk_banks[2][0], BEFORE_NEURONS[0]))
+        neurons(0, starts[0], CHUNKS[0], chunk_banks[0][0])
+        finish(range(BEFORE_NEURONS[0], BEFORE_NEURONS[1]))
+        neurons(0, starts[1], CHUNKS[1], chunk_banks[1][0])
+        finish(range(BEFORE_NEURONS[1], BANKS))
         scale(0, starts[0], CHUNKS[0], POOL_GAINS[0])
         hidden(2)
         scale(0, starts[1], CHUNKS[1], POOL_GAINS[1])
-        waiting = []
 
-        def planes_of(g, m0, width, cut=0):
-            y_bf = round_y(y[g][:, :, m0 : m0 + width], width, cut)
-            if waiting:
-                quantize_y(*waiting.pop())
-            waiting.append((g, m0, width, y_bf))
+        wide = [(1, 0), (0, HALF), (1, HALF)]
+        for n, (g, m0) in enumerate(wide):
+            neurons(g, m0, HALF, (n % 2) * BANKS // 2)
+        for g, m0 in wide:
+            scale(g, m0, HALF)
 
-        neurons(1, 0, HALF)
-        neurons(0, HALF, HALF)
-        neurons(1, HALF, HALF)
-        scale(1, 0, HALF)
-        scale(0, HALF, HALF)
-        scale(1, HALF, HALF)
-        planes_of(0, 0, PIECE)
-        planes_of(0, PIECE, PIECE)
-        planes_of(1, 0, HALF)
-        planes_of(0, HALF, HALF, SCALAR_PAIRS[0])
-        planes_of(1, HALF, PIECE, SCALAR_PAIRS[1])
-        planes_of(1, HALF + PIECE, PIECE, SCALAR_PAIRS[2])
-        quantize_y(*waiting.pop())
+        pieces = [
+            (0, 0, QUARTER, HALF, 0),
+            (0, QUARTER, QUARTER, HALF, 0),
+            (1, 0, HALF, HALF, 0),
+            (0, HALF, HALF, HALF, SCALAR_PAIRS[0]),
+            (1, HALF, QUARTER, QUARTER, SCALAR_PAIRS[1]),
+            (1, HALF + QUARTER, QUARTER, QUARTER, SCALAR_PAIRS[2]),
+        ]
+        waiting = None
+        for g, m0, width, span, scalar_pairs in pieces:
+            y_bf = round_y(g, m0, width, scalar_pairs)
+            if waiting is not None:
+                quantize_y(*waiting)
+            waiting = (g, m0, width, span, y_bf)
+        quantize_y(*waiting)
         for q in range(QUADS):
             nc.scalar.dma_start(
                 out_2[:, PACK * q : PACK * (q + 1), :].rearrange("g r m -> r g m").bitcast(I32),

@@ -32,12 +32,12 @@ TOK = S // BANKS
 QUARTER = S // 4
 FIRST_PAIR, SECOND_PAIR = range(0, 2), range(2, PACK)
 
-CHUNKS = [QUARTER, QUARTER, HALF]
+CHUNKS = [TOK, TOK, QUARTER, HALF]
 POOL_GAINS = [4, 1]
 SCALAR_PAIRS = [256, 96, 112]
 THIRD_VECTOR = 96
-FREED_EARLY = 5
-BEFORE_NEURONS = [5, 7]
+FREED_EARLY = 6
+BEFORE_NEURONS = [4, 5, 7]
 WOVEN_BUFS = 4
 
 
@@ -131,14 +131,21 @@ def tile_list_contextual_sparse_ffn_kernel(
             v2_sc_picked[:].rearrange("p (g m t) -> p g t m", g=GROUPS, t=PACK),
         )
 
+        runs = [HALF] * (PASSES - 1) + [QUARTER]
         v_codes = [
-            [keep.tile([P, HALF], U32, name="v_codes%d_%d" % (a, u), align_bytes=64) for u in range(2)] for a in range(PASSES)
+            [keep.tile([P, runs[a]], U32, name="v_codes%d_%d" % (a, u), align_bytes=64) for u in range(S // runs[a])]
+            for a in range(PASSES)
         ]
-        b_banks = [psum.tile([P, HALF], F32, name="b%d" % c, tag="bank%d" % c) for c in range(BANKS)]
-        half_cols = HALF // LIST_ROWS
+
+        def picked(a, n0, width):
+            u, at = divmod(n0, runs[a])
+            return v_codes[a][u][:, at : at + width].bitcast(FP8X4)
+
+        b_banks = [psum.tile([P, 2, QUARTER], F32, name="b%d" % c, tag="bank%d" % c) for c in range(BANKS)]
         for a in range(PASSES):
-            for u in range(2):
-                nc.vector.tensor_copy(v_codes[a][u][:], tab_w[a][:].indirect(idx[:, u * half_cols : (u + 1) * half_cols]))
+            run_cols = runs[a] // LIST_ROWS
+            for u in range(S // runs[a]):
+                nc.vector.tensor_copy(v_codes[a][u][:], tab_w[a][:].indirect(idx[:, u * run_cols : (u + 1) * run_cols]))
             if a == 0:
                 load_table(PASSES - 1)
                 nc.vector.tensor_copy(v2_picked[:], tab2_w[:].indirect(idx2[:]))
@@ -150,30 +157,30 @@ def tile_list_contextual_sparse_ffn_kernel(
                 load_w1(2 * a - 2)
                 load_w1(2 * a - 1)
             for c in range(BANKS):
-                u, t = divmod(c, PACK)
-                nc.tensor.matmul_mx(
-                    out=b_banks[c][:],
-                    lhsT=w4_codes[a][:, 2 * P * t : 2 * P * (t + 1)].bitcast(FP4X4),
-                    lhsT_scale=planes[:, a, S + P * t : S + P * (t + 1)],
-                    rhs=v_codes[a][u][:].bitcast(FP8X4),
-                    rhs_scale=planes[:, a, u * HALF : (u + 1) * HALF],
-                    start=(a == 0),
-                    stop=(a == PASSES - 1),
-                )
+                quarter, pair = divmod(c, 2)
+                for s in range(2):
+                    t = 2 * pair + s
+                    nc.tensor.matmul_mx(
+                        out=b_banks[c][:, s, :],
+                        lhsT=w4_codes[a][:, 2 * P * t : 2 * P * (t + 1)].bitcast(FP4X4),
+                        lhsT_scale=planes[:, a, S + P * t : S + P * (t + 1)],
+                        rhs=picked(a, quarter * QUARTER, QUARTER),
+                        rhs_scale=planes[:, a, quarter * QUARTER : (quarter + 1) * QUARTER],
+                        start=(a == 0 and s == 0),
+                        stop=(a == PASSES - 1 and s == 1),
+                    )
 
         nc.vector.memset(v2_plane[:].bitcast(I32), 0)
-        for q in range(QUADS):
-            nc.sync.dma_start(
-                v2_plane[QUAD * q : QUAD * q + PACK, :].bitcast(I32),
-                v2_sc_dealt[P - rows + PACK * q : P - rows + PACK * (q + 1), :].bitcast(I32),
-            )
+        for r in range(PACK):
+            nc.sync.dma_start(v2_plane[r:P:QUAD, :].bitcast(I32), v2_sc_dealt[P - rows + r : P : PACK, :].bitcast(I32))
         nc.sync.dma_start(bias[:], bn.rearrange("(g p t) -> p g t", g=GROUPS, t=PACK))
         nc.sync.dma_start(gains[:], gain.rearrange("(g p t) -> p g t", g=GROUPS, t=PACK))
 
         gates = [keep.tile([P, PACK, HALF], F32, name="gate%d" % u) for u in range(2)]
         for c in range(BANKS):
-            u, t = divmod(c, PACK)
-            nc.scalar.activation(gates[u][:, t, :], b_banks[c][:], ACT.Sigmoid)
+            quarter, pair = divmod(c, 2)
+            u, n0 = divmod(quarter * QUARTER, HALF)
+            nc.scalar.activation(gates[u][:, 2 * pair : 2 * pair + 2, n0 : n0 + QUARTER], b_banks[c][:], ACT.Sigmoid)
 
         w1_codes = [keep.tile([P, H], U32, name="w1_codes%d" % a, align_bytes=64) for a in range(PASSES)]
         w1_planes = [keep.tile([P, H], U8, name="w1_plane%d" % a, align_bytes=64) for a in range(PASSES)]
@@ -208,37 +215,36 @@ def tile_list_contextual_sparse_ffn_kernel(
         starts = [sum(CHUNKS[:ci]) for ci in range(len(CHUNKS))]
         chunk_banks = [range(m0 // TOK, (m0 + width) // TOK) for m0, width in zip(starts, CHUNKS)]
 
+        early = range(2)
+
         def project(a, banks, slots=range(PACK)):
             for c in banks:
-                u, n0 = divmod(c * TOK, HALF)
                 first_pass = 0 if c < FREED_EARLY else 1
-                last_pass = 3 if c in chunk_banks[0] else 2
+                last_pass = 3 if c in early else 2
                 for t in slots:
                     nc.tensor.matmul_mx(
                         out=a_banks[c][:, t, :],
                         lhsT=w1_codes[a][:, P * t : P * (t + 1)].bitcast(FP8X4),
                         lhsT_scale=w1_planes[a][:, P * t : P * (t + 1)],
-                        rhs=v_codes[a][u][:, n0 : n0 + TOK].bitcast(FP8X4),
+                        rhs=picked(a, c * TOK, TOK),
                         rhs_scale=planes[:, a, c * TOK : (c + 1) * TOK],
                         start=(a == first_pass and t == 0),
                         stop=(a == last_pass and t == PACK - 1),
                     )
 
-        for banks in (chunk_banks[0], range(len(chunk_banks[0]), FREED_EARLY)):
+        for banks in (early, range(len(early), FREED_EARLY)):
             project(0, banks, FIRST_PAIR)
             project(0, banks, SECOND_PAIR)
         project(1, range(BANKS), FIRST_PAIR)
         project(1, range(BANKS), SECOND_PAIR)
-        project(0, range(FREED_EARLY, BANKS - 1))
-        project(2, chunk_banks[0])
-        project(3, chunk_banks[0], FIRST_PAIR)
-        project(3, chunk_banks[0], SECOND_PAIR)
+        project(0, range(FREED_EARLY, BANKS))
+        project(2, early)
+        project(3, early, FIRST_PAIR)
+        project(3, early, SECOND_PAIR)
 
         def finish(banks):
             for c in banks:
                 project(3, [c])
-                if c == BANKS - 1:
-                    project(0, [c])
                 project(2, [c])
 
         h_bf = late.tile([P, S * PACK], BF16, name="h_bf", align_bytes=64)
@@ -317,17 +323,16 @@ def tile_list_contextual_sparse_ffn_kernel(
                     y_codes[g][:, lo : lo + span].bitcast(I32),
                 )
 
-        hidden(0)
-        finish(chunk_banks[1])
-        hidden(1)
-        finish(range(chunk_banks[2][0], BEFORE_NEURONS[0]))
-        neurons(0, starts[0], CHUNKS[0], chunk_banks[0][0])
-        finish(range(BEFORE_NEURONS[0], BEFORE_NEURONS[1]))
-        neurons(0, starts[1], CHUNKS[1], chunk_banks[1][0])
-        finish(range(BEFORE_NEURONS[1], BANKS))
-        scale(0, starts[0], CHUNKS[0], POOL_GAINS[0])
-        hidden(2)
-        scale(0, starts[1], CHUNKS[1], POOL_GAINS[1])
+        done = len(early)
+        for ci, ahead in enumerate(BEFORE_NEURONS):
+            finish(range(done, ahead))
+            done = ahead
+            hidden(ci)
+            neurons(0, starts[ci], CHUNKS[ci], chunk_banks[ci][0])
+        finish(range(done, BANKS))
+        scale(0, 0, QUARTER, POOL_GAINS[0])
+        hidden(len(CHUNKS) - 1)
+        scale(0, QUARTER, QUARTER, POOL_GAINS[1])
 
         wide = [(1, 0), (0, HALF), (1, HALF)]
         for n, (g, m0) in enumerate(wide):
@@ -350,8 +355,7 @@ def tile_list_contextual_sparse_ffn_kernel(
                 quantize_y(*waiting)
             waiting = (g, m0, width, span, y_bf)
         quantize_y(*waiting)
-        for q in range(QUADS):
-            nc.scalar.dma_start(
-                out_2[:, PACK * q : PACK * (q + 1), :].rearrange("g r m -> r g m").bitcast(I32),
-                y_planes[QUAD * q : QUAD * q + PACK, :, :].bitcast(I32),
+        for r in range(PACK):
+            (nc.scalar, nc.sync)[r % 2].dma_start(
+                out_2[:, r::PACK, :].rearrange("g q m -> q g m").bitcast(I32), y_planes[r:P:QUAD, :, :].bitcast(I32)
             )

@@ -33,7 +33,7 @@ QUARTER = S // 4
 FIRST_PAIR, SECOND_PAIR = range(0, 2), range(2, PACK)
 
 CHUNKS = [TOK, TOK, QUARTER, HALF]
-POOL_GAINS = [4, 1]
+POOL_GAINS = [2, 2]
 SCALAR_PAIRS = [256, 96, 112]
 THIRD_VECTOR = 96
 FREED_EARLY = 6
@@ -292,9 +292,9 @@ def tile_list_contextual_sparse_ffn_kernel(
                     t = t0 + s
                     nc.scalar.activation(y[g][:, t, cols], z[:, s, :], ACT.Gelu_apprx_tanh, bias=bias[:, g, t : t + 1])
 
-        def scale(g, m0, width, pool_gains=0):
+        def scale(g, m0, width, pool_gains=0, slots=range(PACK)):
             cols = slice(m0, m0 + width)
-            for t in range(PACK):
+            for t in slots:
                 if t < pool_gains:
                     nc.gpsimd.tensor_scalar(y[g][:, t, cols], y[g][:, t, cols], gains[:, g, t : t + 1], 0.0, MULT, ADD)
                 else:
@@ -327,18 +327,21 @@ def tile_list_contextual_sparse_ffn_kernel(
         for ci, ahead in enumerate(BEFORE_NEURONS):
             finish(range(done, ahead))
             done = ahead
+            if ci == 2:
+                scale(0, 0, QUARTER, POOL_GAINS[0])
             hidden(ci)
             neurons(0, starts[ci], CHUNKS[ci], chunk_banks[ci][0])
         finish(range(done, BANKS))
-        scale(0, 0, QUARTER, POOL_GAINS[0])
-        hidden(len(CHUNKS) - 1)
-        scale(0, QUARTER, QUARTER, POOL_GAINS[1])
 
-        wide = [(1, 0), (0, HALF), (1, HALF)]
-        for n, (g, m0) in enumerate(wide):
-            neurons(g, m0, HALF, (n % 2) * BANKS // 2)
-        for g, m0 in wide:
-            scale(g, m0, HALF)
+        scale(0, QUARTER, QUARTER, POOL_GAINS[1])
+        neurons(1, 0, HALF, 0)
+        scale(1, 0, HALF, slots=FIRST_PAIR)
+        hidden(len(CHUNKS) - 1)
+        neurons(0, HALF, HALF, BANKS // 2)
+        neurons(1, HALF, HALF, 0)
+        scale(1, 0, HALF, slots=SECOND_PAIR)
+        scale(0, HALF, HALF)
+        scale(1, HALF, HALF)
 
         pieces = [
             (0, 0, QUARTER, HALF, 0),

@@ -35,7 +35,7 @@ FIRST_PAIR, SECOND_PAIR = range(0, 2), range(2, PACK)
 CHUNKS = [TOK, TOK, QUARTER, HALF]
 POOL_GAINS = [2, 2]
 SCALAR_PAIRS = [256, 96, 112]
-THIRD_VECTOR = 96
+THIRD_VECTOR = 80
 FREED_EARLY = 6
 BEFORE_NEURONS = [4, 5, 7]
 WOVEN_BUFS = 4
@@ -196,11 +196,10 @@ def tile_list_contextual_sparse_ffn_kernel(
                 nc.vector.tensor_copy(dealt[:, 0:THIRD_VECTOR], whole[:, 0:THIRD_VECTOR])
                 nc.scalar.copy(dealt[:, THIRD_VECTOR:], whole[:, THIRD_VECTOR:])
             else:
-                for u in range(2):
-                    half = w1_last[u][:].rearrange("p j (m t) -> p m j t", t=PACK)
-                    places = slice(u * P // 2, (u + 1) * P // 2)
-                    nc.vector.tensor_copy(dealt[:, places, :, 0:2], half[:, :, :, 0:2])
-                    nc.scalar.copy(dealt[:, places, :, 2:PACK], half[:, :, :, 2:PACK])
+                halves = [w1_last[u][:].rearrange("p j (m t) -> p m j t", t=PACK) for u in range(2)]
+                nc.scalar.copy(dealt[:, 0 : P // 2], halves[0])
+                nc.vector.tensor_copy(dealt[:, P // 2 :, :, 0:2], halves[1][:, :, :, 0:2])
+                nc.scalar.copy(dealt[:, P // 2 :, :, 2:PACK], halves[1][:, :, :, 2:PACK])
             calls = 1 if a == PASSES - 2 else 2
             for u in range(calls):
                 cols = slice(u * H // calls, (u + 1) * H // calls)

@@ -33,7 +33,7 @@ QUARTER = S // 4
 FIRST_PAIR, SECOND_PAIR = range(0, 2), range(2, PACK)
 
 CHUNKS = [TOK, TOK, QUARTER, HALF]
-POOL_GAINS = [2, 2]
+POOL_GAINS = [2, 0]
 SCALAR_PAIRS = [256, 96, 112]
 THIRD_VECTOR = 80
 FREED_EARLY = 6

@@ -19,21 +19,25 @@ ADD = mybir.AluOpType.add
 
 P = 128
 PACK = 4
+SLOTS = PACK
 K_PASS = P * PACK
 PASSES = K // K_PASS
 GROUPS = S2 // K_PASS
 QUADS = 4
 QUAD = P // QUADS
+QUAD_ROWS = 4
+PLANE_ROWS = QUADS * QUAD_ROWS
+STAGED_ROWS = QUAD_ROWS * PASSES
 LIST_ROWS = 16
 BANKS = 8
 BANK_F32 = 512
 HALF = S // 2
-TOK = S // BANKS
 QUARTER = S // 4
-FIRST_PAIR, SECOND_PAIR = range(0, 2), range(2, PACK)
+TOK = S // BANKS
+FIRST_PAIR, SECOND_PAIR = range(0, 2), range(2, SLOTS)
 
 CHUNKS = [TOK, TOK, QUARTER, HALF]
-POOL_GAINS = [2, 0]
+POOL_GAINS = 2
 SCALAR_PAIRS = [256, 96, 112]
 THIRD_VECTOR = 80
 FREED_EARLY = 6
@@ -69,9 +73,8 @@ def tile_list_contextual_sparse_ffn_kernel(
         tab2_w = keep.tile([P, T2], U32, name="tab2_w", align_bytes=64)
         planes = keep.tile([P, PASSES, S + H], U8, name="planes", align_bytes=64)
         v2_plane = shared.tile([P, S2], U8, name="v2_plane", offset=0, align_bytes=64)
-        bias = shared.tile([P, GROUPS, PACK], F32, name="bias", offset=S2)
-        gains = shared.tile([P, GROUPS, PACK], F32, name="gains", offset=S2 + 64)
-        rows = PACK * PASSES
+        bias = shared.tile([P, GROUPS, SLOTS], F32, name="bias", offset=S2)
+        gains = shared.tile([P, GROUPS, SLOTS], F32, name="gains", offset=S2 + 64)
 
         def load_table(a):
             nc.sync.dma_start(tab_w[a][:].bitcast(I32), tab_words[a].rearrange("p n i -> p (n i)").bitcast(I32))
@@ -89,35 +92,35 @@ def tile_list_contextual_sparse_ffn_kernel(
         nc.sync.dma_start(w4_sc_raw[QUAD : P - QUAD, :].bitcast(I32), w4_scales.rearrange("a q n -> q a n").bitcast(I32))
         nc.sync.dma_start(w4_raw[:].bitcast(I32), w4_words.rearrange("a p n -> p a n").bitcast(I32))
         nc.sync.dma_start(idx2[:], offs2)
-        nc.sync.dma_start(tab2_sc[P - rows :, :].bitcast(I32), tab2_scales[0].bitcast(I32))
+        nc.sync.dma_start(tab2_sc[P - PLANE_ROWS :, :].bitcast(I32), tab2_scales[0].bitcast(I32))
         load_table(0)
         nc.sync.dma_start(tab2_w[:].bitcast(I32), tab2_words[0].rearrange("p n i -> p (n i)").bitcast(I32))
 
         for raw in (tab_sc, w4_sc_raw):
             nc.vector.memset(raw[0:QUAD, :].bitcast(I32), 0)
             nc.vector.memset(raw[P - QUAD :, :].bitcast(I32), 0)
-        nc.vector.memset(tab2_sc[0 : P - rows, :].bitcast(I32), 0)
+        nc.vector.memset(tab2_sc[0 : P - PLANE_ROWS, :].bitcast(I32), 0)
         nc.vector.memset(planes[:].bitcast(I32), 0)
 
         v_sc_picked = shared.tile([P, S], U8, name="v_sc_picked", offset=region + T)
         staged = keep.tile([P, S + H], U8, name="staged", align_bytes=64)
         nc.vector.tensor_copy(v_sc_picked[:], tab_sc[:].indirect(idx[:]))
         nc.vector.tensor_copy(
-            staged[:, S:].rearrange("p (t m) -> p t m", t=PACK), w4_sc_raw[:].rearrange("p (m t) -> p t m", t=PACK)
+            staged[:, S:].rearrange("p (t m) -> p t m", t=SLOTS), w4_sc_raw[:].rearrange("p (m t) -> p t m", t=SLOTS)
         )
         nc.vector.tensor_copy(staged[:, 0:S].bitcast(I32), v_sc_picked[:].bitcast(I32))
-        for q in (0, 2, 1, 3):
+        for quad in (0, 2, 1, 3):
             nc.scalar.dma_start(
-                planes[QUAD * q : QUAD * q + PACK, :, :].bitcast(I32),
-                staged[QUAD + rows * q : QUAD + rows * (q + 1), :].bitcast(I32),
+                planes[QUAD * quad : QUAD * quad + QUAD_ROWS, :, :].bitcast(I32),
+                staged[QUAD + STAGED_ROWS * quad : QUAD + STAGED_ROWS * (quad + 1), :].bitcast(I32),
             )
         load_table(1)
 
         w4_codes = [keep.tile([P, 2 * H], U8, name="w4_codes%d" % a, align_bytes=64) for a in range(PASSES)]
         for a in range(PASSES):
             nc.vector.tensor_copy(
-                w4_codes[a][:].bitcast(U16).rearrange("p (t m) -> p t m", t=PACK),
-                w4_raw[:, a, :].bitcast(U16).rearrange("p (m t) -> p t m", t=PACK),
+                w4_codes[a][:].bitcast(U16).rearrange("p (t m) -> p t m", t=SLOTS),
+                w4_raw[:, a, :].bitcast(U16).rearrange("p (m t) -> p t m", t=SLOTS),
             )
         load_table(2)
 
@@ -127,8 +130,8 @@ def tile_list_contextual_sparse_ffn_kernel(
         v2_sc_dealt = keep.tile([P, S2], U8, name="v2_sc_dealt", align_bytes=64)
         nc.vector.tensor_copy(v2_sc_picked[:], tab2_sc[:].indirect(idx2[:]))
         nc.vector.tensor_copy(
-            v2_sc_dealt[:].rearrange("p (g t m) -> p g t m", g=GROUPS, t=PACK),
-            v2_sc_picked[:].rearrange("p (g m t) -> p g t m", g=GROUPS, t=PACK),
+            v2_sc_dealt[:].rearrange("p (g t m) -> p g t m", g=GROUPS, t=SLOTS),
+            v2_sc_picked[:].rearrange("p (g m t) -> p g t m", g=GROUPS, t=SLOTS),
         )
 
         runs = [HALF] * (PASSES - 1) + [QUARTER]
@@ -141,7 +144,7 @@ def tile_list_contextual_sparse_ffn_kernel(
             u, at = divmod(n0, runs[a])
             return v_codes[a][u][:, at : at + width].bitcast(FP8X4)
 
-        b_banks = [psum.tile([P, 2, QUARTER], F32, name="b%d" % c, tag="bank%d" % c) for c in range(BANKS)]
+        gate_banks = [psum.tile([P, 2, QUARTER], F32, name="b%d" % c, tag="bank%d" % c) for c in range(BANKS)]
         for a in range(PASSES):
             run_cols = runs[a] // LIST_ROWS
             for u in range(S // runs[a]):
@@ -150,8 +153,8 @@ def tile_list_contextual_sparse_ffn_kernel(
                 load_table(PASSES - 1)
                 nc.vector.tensor_copy(v2_picked[:], tab2_w[:].indirect(idx2[:]))
                 nc.vector.tensor_copy(
-                    v2_codes[:].bitcast(I32).rearrange("p (g t b i) -> p g b t i", g=GROUPS, t=PACK, i=PACK),
-                    v2_picked[:].bitcast(I32).rearrange("p (g b i t) -> p g b t i", g=GROUPS, t=PACK, i=PACK),
+                    v2_codes[:].bitcast(I32).rearrange("p (g t b i) -> p g b t i", g=GROUPS, t=SLOTS, i=PACK),
+                    v2_picked[:].bitcast(I32).rearrange("p (g b i t) -> p g b t i", g=GROUPS, t=SLOTS, i=PACK),
                 )
             if a in (1, 2):
                 load_w1(2 * a - 2)
@@ -161,7 +164,7 @@ def tile_list_contextual_sparse_ffn_kernel(
                 for s in range(2):
                     t = 2 * pair + s
                     nc.tensor.matmul_mx(
-                        out=b_banks[c][:, s, :],
+                        out=gate_banks[c][:, s, :],
                         lhsT=w4_codes[a][:, 2 * P * t : 2 * P * (t + 1)].bitcast(FP4X4),
                         lhsT_scale=planes[:, a, S + P * t : S + P * (t + 1)],
                         rhs=picked(a, quarter * QUARTER, QUARTER),
@@ -171,35 +174,41 @@ def tile_list_contextual_sparse_ffn_kernel(
                     )
 
         nc.vector.memset(v2_plane[:].bitcast(I32), 0)
-        for r in range(PACK):
-            nc.sync.dma_start(v2_plane[r:P:QUAD, :].bitcast(I32), v2_sc_dealt[P - rows + r : P : PACK, :].bitcast(I32))
-        nc.sync.dma_start(bias[:], bn.rearrange("(g p t) -> p g t", g=GROUPS, t=PACK))
-        nc.sync.dma_start(gains[:], gain.rearrange("(g p t) -> p g t", g=GROUPS, t=PACK))
+        for r in range(QUAD_ROWS):
+            nc.sync.dma_start(
+                v2_plane[r:P:QUAD, :].bitcast(I32), v2_sc_dealt[P - PLANE_ROWS + r : P : QUAD_ROWS, :].bitcast(I32)
+            )
+        nc.sync.dma_start(bias[:], bn.rearrange("(g p t) -> p g t", g=GROUPS, t=SLOTS))
+        nc.sync.dma_start(gains[:], gain.rearrange("(g p t) -> p g t", g=GROUPS, t=SLOTS))
 
-        gates = [keep.tile([P, PACK, HALF], F32, name="gate%d" % u) for u in range(2)]
+        gates = [keep.tile([P, SLOTS, HALF], F32, name="gate%d" % u) for u in range(2)]
         for c in range(BANKS):
             quarter, pair = divmod(c, 2)
             u, n0 = divmod(quarter * QUARTER, HALF)
-            nc.scalar.activation(gates[u][:, 2 * pair : 2 * pair + 2, n0 : n0 + QUARTER], b_banks[c][:], ACT.Sigmoid)
+            nc.scalar.activation(gates[u][:, 2 * pair : 2 * pair + 2, n0 : n0 + QUARTER], gate_banks[c][:], ACT.Sigmoid)
 
-        w1_codes = [keep.tile([P, H], U32, name="w1_codes%d" % a, align_bytes=64) for a in range(PASSES)]
-        w1_planes = [keep.tile([P, H], U8, name="w1_plane%d" % a, align_bytes=64) for a in range(PASSES)]
+        stationary = ctx.enter_context(tc.tile_pool(name="stationary", bufs=1))
+        pitch = H * 4 + H + 256
+        w1_codes = [
+            stationary.tile([P, H], U32, name="w1_codes%d" % a, offset=a * pitch + 128 + H, align_bytes=64) for a in range(PASSES)
+        ]
+        w1_planes = [stationary.tile([P, H], U8, name="w1_plane%d" % a, offset=a * pitch + 64, align_bytes=64) for a in range(PASSES)]
         for a in range(PASSES):
             w1_bf = ring.tile([P, H * PACK], BF16, name="woven", align_bytes=64)
-            dealt = w1_bf[:].rearrange("p (t m j) -> p m j t", t=PACK, j=PACK)
+            dealt = w1_bf[:].rearrange("p (t m j) -> p m j t", t=SLOTS, j=PACK)
             if a < PASSES - 2:
-                whole = w1_raw[a][:].rearrange("p j (m t) -> p m j t", t=PACK)
+                whole = w1_raw[a][:].rearrange("p j (m t) -> p m j t", t=SLOTS)
                 for u in range(2):
                     nc.vector.tensor_copy(dealt[:, :, :, 2 * u : 2 * u + 2], whole[:, :, :, 2 * u : 2 * u + 2])
             elif a == PASSES - 2:
-                whole = w1_raw[a][:].rearrange("p j (m t) -> p m j t", t=PACK)
+                whole = w1_raw[a][:].rearrange("p j (m t) -> p m j t", t=SLOTS)
                 nc.vector.tensor_copy(dealt[:, 0:THIRD_VECTOR], whole[:, 0:THIRD_VECTOR])
                 nc.scalar.copy(dealt[:, THIRD_VECTOR:], whole[:, THIRD_VECTOR:])
             else:
-                halves = [w1_last[u][:].rearrange("p j (m t) -> p m j t", t=PACK) for u in range(2)]
+                halves = [w1_last[u][:].rearrange("p j (m t) -> p m j t", t=SLOTS) for u in range(2)]
                 nc.scalar.copy(dealt[:, 0 : P // 2], halves[0])
                 nc.vector.tensor_copy(dealt[:, P // 2 :, :, 0:2], halves[1][:, :, :, 0:2])
-                nc.scalar.copy(dealt[:, P // 2 :, :, 2:PACK], halves[1][:, :, :, 2:PACK])
+                nc.scalar.copy(dealt[:, P // 2 :, :, 2:SLOTS], halves[1][:, :, :, 2:SLOTS])
             calls = 1 if a == PASSES - 2 else 2
             for u in range(calls):
                 cols = slice(u * H // calls, (u + 1) * H // calls)
@@ -210,25 +219,25 @@ def tile_list_contextual_sparse_ffn_kernel(
                 )
 
         late = ctx.enter_context(tc.tile_pool(name="late", bufs=1))
-        a_banks = [psum.tile([P, PACK, TOK], F32, name="a%d" % c, tag="bank%d" % c) for c in range(BANKS)]
+        proj_banks = [psum.tile([P, SLOTS, TOK], F32, name="a%d" % c, tag="bank%d" % c) for c in range(BANKS)]
         starts = [sum(CHUNKS[:ci]) for ci in range(len(CHUNKS))]
         chunk_banks = [range(m0 // TOK, (m0 + width) // TOK) for m0, width in zip(starts, CHUNKS)]
 
         early = range(2)
 
-        def project(a, banks, slots=range(PACK)):
+        def project(a, banks, slots=range(SLOTS)):
             for c in banks:
                 first_pass = 0 if c < FREED_EARLY else 1
-                last_pass = 3 if c in early else 2
+                last_pass = PASSES - 1 if c in early else PASSES - 2
                 for t in slots:
                     nc.tensor.matmul_mx(
-                        out=a_banks[c][:, t, :],
+                        out=proj_banks[c][:, t, :],
                         lhsT=w1_codes[a][:, P * t : P * (t + 1)].bitcast(FP8X4),
                         lhsT_scale=w1_planes[a][:, P * t : P * (t + 1)],
                         rhs=picked(a, c * TOK, TOK),
                         rhs_scale=planes[:, a, c * TOK : (c + 1) * TOK],
                         start=(a == first_pass and t == 0),
-                        stop=(a == last_pass and t == PACK - 1),
+                        stop=(a == last_pass and t == SLOTS - 1),
                     )
 
         for banks in (early, range(len(early), FREED_EARLY)):
@@ -254,8 +263,8 @@ def tile_list_contextual_sparse_ffn_kernel(
             for c in chunk_banks[ci]:
                 u, n0 = divmod(c * TOK, HALF)
                 nc.vector.tensor_tensor(
-                    h_bf[:, c * TOK * PACK : (c + 1) * TOK * PACK].rearrange("p (n i t) -> p n t i", t=PACK, i=2),
-                    a_banks[c][:].rearrange("p t (n i) -> p n t i", i=2),
+                    h_bf[:, c * TOK * PACK : (c + 1) * TOK * PACK].rearrange("p (n i t) -> p n t i", t=SLOTS, i=2),
+                    proj_banks[c][:].rearrange("p t (n i) -> p n t i", i=2),
                     gates[u][:, :, n0 : n0 + TOK].rearrange("p t (n i) -> p n t i", i=2),
                     MULT,
                 )
@@ -266,15 +275,15 @@ def tile_list_contextual_sparse_ffn_kernel(
                 in_=h_bf[:, m0 * PACK : (m0 + width) * PACK],
             )
 
-        y = [late.tile([P, PACK, S], F32, name="y%d" % g, align_bytes=64) for g in range(GROUPS)]
+        y = [late.tile([P, SLOTS, S], F32, name="y%d" % g, align_bytes=64) for g in range(GROUPS)]
         y_codes = [late.tile([P, S], U32, name="y_codes%d" % g, align_bytes=64) for g in range(GROUPS)]
         y_planes = late.tile([P, GROUPS, S], U8, name="y_planes", align_bytes=64)
-        rows_out = [out_0[K_PASS * g : K_PASS * (g + 1), :].rearrange("(p t) m -> p t m", t=PACK) for g in range(GROUPS)]
+        rows_out = [out_0[K_PASS * g : K_PASS * (g + 1), :].rearrange("(p t) m -> p t m", t=SLOTS) for g in range(GROUPS)]
 
         def neurons(g, m0, width, bank0):
             per_bank = BANK_F32 // width
             cols = slice(m0, m0 + width)
-            for t0 in range(0, PACK, per_bank):
+            for t0 in range(0, SLOTS, per_bank):
                 z = psum.tile([P, per_bank, width], F32, name="z%d_%d_%d" % (g, m0, t0), tag="bank%d" % (bank0 + t0 // per_bank))
                 for s in range(per_bank):
                     col = K_PASS * g + P * (t0 + s)
@@ -291,7 +300,7 @@ def tile_list_contextual_sparse_ffn_kernel(
                     t = t0 + s
                     nc.scalar.activation(y[g][:, t, cols], z[:, s, :], ACT.Gelu_apprx_tanh, bias=bias[:, g, t : t + 1])
 
-        def scale(g, m0, width, pool_gains=0, slots=range(PACK)):
+        def scale(g, m0, width, pool_gains=0, slots=range(SLOTS)):
             cols = slice(m0, m0 + width)
             for t in slots:
                 if t < pool_gains:
@@ -303,7 +312,7 @@ def tile_list_contextual_sparse_ffn_kernel(
 
         def round_y(g, m0, width, scalar_pairs):
             y_bf = ring.tile([P, width * PACK], BF16, name="woven", align_bytes=64)
-            woven = y_bf[:].rearrange("p (n i t) -> p n t i", t=PACK, i=2)
+            woven = y_bf[:].rearrange("p (n i t) -> p n t i", t=SLOTS, i=2)
             apart = y[g][:, :, m0 : m0 + width].rearrange("p t (n i) -> p n t i", i=2)
             if scalar_pairs > 0:
                 nc.scalar.copy(woven[:, 0:scalar_pairs], apart[:, 0:scalar_pairs])
@@ -326,13 +335,13 @@ def tile_list_contextual_sparse_ffn_kernel(
         for ci, ahead in enumerate(BEFORE_NEURONS):
             finish(range(done, ahead))
             done = ahead
-            if ci == 2:
-                scale(0, 0, QUARTER, POOL_GAINS[0])
+            if starts[ci] == QUARTER:
+                scale(0, 0, QUARTER, POOL_GAINS)
             hidden(ci)
             neurons(0, starts[ci], CHUNKS[ci], chunk_banks[ci][0])
         finish(range(done, BANKS))
 
-        scale(0, QUARTER, QUARTER, POOL_GAINS[1])
+        scale(0, QUARTER, QUARTER)
         neurons(1, 0, HALF, 0)
         scale(1, 0, HALF, slots=FIRST_PAIR)
         hidden(len(CHUNKS) - 1)
@@ -357,7 +366,7 @@ def tile_list_contextual_sparse_ffn_kernel(
                 quantize_y(*waiting)
             waiting = (g, m0, width, span, y_bf)
         quantize_y(*waiting)
-        for r in range(PACK):
+        for r in range(QUAD_ROWS):
             (nc.scalar, nc.sync)[r % 2].dma_start(
-                out_2[:, r::PACK, :].rearrange("g q m -> q g m").bitcast(I32), y_planes[r:P:QUAD, :, :].bitcast(I32)
+                out_2[:, r::QUAD_ROWS, :].rearrange("g q m -> q g m").bitcast(I32), y_planes[r:P:QUAD, :, :].bitcast(I32)
             )

@@ -72,9 +72,9 @@ def tile_list_contextual_sparse_ffn_kernel(
         tab2_sc = keep.tile([P, T2], U8, name="tab2_sc", align_bytes=64)
         tab2_w = keep.tile([P, T2], U32, name="tab2_w", align_bytes=64)
         planes = keep.tile([P, PASSES, S + H], U8, name="planes", align_bytes=64)
-        v2_plane = shared.tile([P, S2], U8, name="v2_plane", offset=0, align_bytes=64)
-        bias = shared.tile([P, GROUPS, SLOTS], F32, name="bias", offset=S2)
-        gains = shared.tile([P, GROUPS, SLOTS], F32, name="gains", offset=S2 + 64)
+        v2_plane = shared.tile([P, S2], U8, name="v2_plane", offset=64, align_bytes=64)
+        bias = shared.tile([P, GROUPS, SLOTS], F32, name="bias", offset=S2 + 64)
+        gains = shared.tile([P, GROUPS, SLOTS], F32, name="gains", offset=S2 + 128)
 
         def load_table(a):
             nc.sync.dma_start(tab_w[a][:].bitcast(I32), tab_words[a].rearrange("p n i -> p (n i)").bitcast(I32))
@@ -124,8 +124,11 @@ def tile_list_contextual_sparse_ffn_kernel(
             )
         load_table(2)
 
+        stationary = ctx.enter_context(tc.tile_pool(name="stationary", bufs=1))
+        pitch = H * 4 + H + 256
+
         v2_picked = keep.tile([P, S2], U32, name="v2_picked", align_bytes=64)
-        v2_codes = keep.tile([P, S2], U32, name="v2_codes", align_bytes=64)
+        v2_codes = stationary.tile([P, S2], U32, name="v2_codes", offset=PASSES * pitch + 128, align_bytes=64)
         v2_sc_picked = keep.tile([P, S2], U8, name="v2_sc_picked", align_bytes=64)
         v2_sc_dealt = keep.tile([P, S2], U8, name="v2_sc_dealt", align_bytes=64)
         nc.vector.tensor_copy(v2_sc_picked[:], tab2_sc[:].indirect(idx2[:]))
@@ -187,8 +190,6 @@ def tile_list_contextual_sparse_ffn_kernel(
             u, n0 = divmod(quarter * QUARTER, HALF)
             nc.scalar.activation(gates[u][:, 2 * pair : 2 * pair + 2, n0 : n0 + QUARTER], gate_banks[c][:], ACT.Sigmoid)
 
-        stationary = ctx.enter_context(tc.tile_pool(name="stationary", bufs=1))
-        pitch = H * 4 + H + 256
         w1_codes = [
             stationary.tile([P, H], U32, name="w1_codes%d" % a, offset=a * pitch + 128 + H, align_bytes=64) for a in range(PASSES)
         ]

from contextlib import ExitStack

import concourse.mybir as mybir

K, T, H, S, T2, S2 = 2048, 4096, 512, 1024, 2048, 1024
FLOPS = 2 * (2 * K * H * S + H * S2 * S)

F32 = mybir.dt.float32
BF16 = mybir.dt.bfloat16
I32 = mybir.dt.int32
U32 = mybir.dt.uint32
U16 = mybir.dt.uint16
U8 = mybir.dt.uint8
FP8X4 = mybir.dt.float8_e4m3fn_x4
FP4X4 = mybir.dt.float4_e2m1fn_x4
ACT = mybir.ActivationFunctionType
MULT = mybir.AluOpType.mult
ADD = mybir.AluOpType.add

P = 128
PACK = 4
SLOTS = PACK
K_PASS = P * PACK
PASSES = K // K_PASS
GROUPS = S2 // K_PASS
QUADS = 4
QUAD = P // QUADS
QUAD_ROWS = 4
PLANE_ROWS = QUADS * QUAD_ROWS
STAGED_ROWS = QUAD_ROWS * PASSES
LIST_ROWS = 16
BANKS = 8
BANK_F32 = 512
HALF = S // 2
QUARTER = S // 4
TOK = S // BANKS
FIRST_PAIR, SECOND_PAIR = range(0, 2), range(2, SLOTS)

CHUNKS = [TOK, TOK, QUARTER, HALF]
POOL_GAINS = 2
SCALAR_PAIRS = [256, 96, 112]
THIRD_VECTOR = 80
FREED_EARLY = 6
BEFORE_NEURONS = [4, 5, 7]
WOVEN_BUFS = 4


def tile_list_contextual_sparse_ffn_kernel(
    tc, tab_words, tab_scales, tab2_words, tab2_scales, w4_words, w4_scales, w1, bn, gain, offs, offs2, out_0, out_1, out_2
):
    nc = tc.nc
    with ExitStack() as ctx:
        lists = ctx.enter_context(tc.tile_pool(name="lists", bufs=1))
        keep = ctx.enter_context(tc.tile_pool(name="keep", bufs=1))
        ring = ctx.enter_context(tc.tile_pool(name="ring", bufs=WOVEN_BUFS))
        psum = ctx.enter_context(tc.psum_pool(name="psum", bufs=1))

        idx = lists.tile([P, S // LIST_ROWS], U16, name="idx")
        idx2 = lists.tile([P, S2 // LIST_ROWS], U16, name="idx2")

        shared = ctx.enter_context(tc.tile_pool(name="shared", bufs=1))
        region = T * 4
        tab_sc = shared.tile([P, T], U8, name="tab_sc", offset=region)
        w4_raw = shared.tile([P, PASSES, 2 * H], U8, name="w4_raw", offset=2 * region)
        tab_w = [shared.tile([P, T], U32, name="tab_w%d" % a, offset=(a % 3) * region) for a in range(PASSES)]
        w1_raw = [shared.tile([P, PACK, H], F32, name="w1_raw%d" % a, offset=region + a * region // 2) for a in range(PASSES - 1)]
        w1_last = [
            shared.tile([P, PACK, H // 2], F32, name="w1_last%d" % u, offset=region + (2 * (PASSES - 1) + u) * region // 4)
            for u in range(2)
        ]
        w4_sc_raw = keep.tile([P, H], U8, name="w4_sc_raw", align_bytes=64)
        tab2_sc = keep.tile([P, T2], U8, name="tab2_sc", align_bytes=64)
        tab2_w = keep.tile([P, T2], U32, name="tab2_w", align_bytes=64)
        planes = keep.tile([P, PASSES, S + H], U8, name="planes", align_bytes=64)
        v2_plane = shared.tile([P, S2], U8, name="v2_plane", offset=64, align_bytes=64)
        bias = shared.tile([P, GROUPS, SLOTS], F32, name="bias", offset=S2 + 64)
        gains = shared.tile([P, GROUPS, SLOTS], F32, name="gains", offset=S2 + 128)

        def load_table(a):
            nc.sync.dma_start(tab_w[a][:].bitcast(I32), tab_words[a].rearrange("p n i -> p (n i)").bitcast(I32))

        def load_w1(a):
            k_rows = w1[K_PASS * a : K_PASS * (a + 1), :].rearrange("(p j) c -> p j c", j=PACK)
            if a < PASSES - 1:
                nc.sync.dma_start(w1_raw[a][:], k_rows)
            else:
                for u in range(2):
                    nc.sync.dma_start(w1_last[u][:], k_rows[:, :, u * H // 2 : (u + 1) * H // 2])

        nc.sync.dma_start(idx[:], offs)
        nc.sync.dma_start(tab_sc[QUAD : P - QUAD, :].bitcast(I32), tab_scales.rearrange("a q n -> q a n").bitcast(I32))
        nc.sync.dma_start(w4_sc_raw[QUAD : P - QUAD, :].bitcast(I32), w4_scales.rearrange("a q n -> q a n").bitcast(I32))
        nc.sync.dma_start(w4_raw[:].bitcast(I32), w4_words.rearrange("a p n -> p a n").bitcast(I32))
        nc.sync.dma_start(idx2[:], offs2)
        nc.sync.dma_start(tab2_sc[P - PLANE_ROWS :, :].bitcast(I32), tab2_scales[0].bitcast(I32))
        load_table(0)
        nc.sync.dma_start(tab2_w[:].bitcast(I32), tab2_words[0].rearrange("p n i -> p (n i)").bitcast(I32))

        for raw in (tab_sc, w4_sc_raw):
            nc.vector.memset(raw[0:QUAD, :].bitcast(I32), 0)
            nc.vector.memset(raw[P - QUAD :, :].bitcast(I32), 0)
        nc.vector.memset(tab2_sc[0 : P - PLANE_ROWS, :].bitcast(I32), 0)
        nc.vector.memset(planes[:].bitcast(I32), 0)

        v_sc_picked = shared.tile([P, S], U8, name="v_sc_picked", offset=region + T)
        staged = keep.tile([P, S + H], U8, name="staged", align_bytes=64)
        nc.vector.tensor_copy(v_sc_picked[:], tab_sc[:].indirect(idx[:]))
        nc.vector.tensor_copy(
            staged[:, S:].rearrange("p (t m) -> p t m", t=SLOTS), w4_sc_raw[:].rearrange("p (m t) -> p t m", t=SLOTS)
        )
        nc.vector.tensor_copy(staged[:, 0:S].bitcast(I32), v_sc_picked[:].bitcast(I32))
        for quad in (0, 2, 1, 3):
            nc.scalar.dma_start(
                planes[QUAD * quad : QUAD * quad + QUAD_ROWS, :, :].bitcast(I32),
                staged[QUAD + STAGED_ROWS * quad : QUAD + STAGED_ROWS * (quad + 1), :].bitcast(I32),
            )
        load_table(1)

        w4_codes = [keep.tile([P, 2 * H], U8, name="w4_codes%d" % a, align_bytes=64) for a in range(PASSES)]
        for a in range(PASSES):
            nc.vector.tensor_copy(
                w4_codes[a][:].bitcast(U16).rearrange("p (t m) -> p t m", t=SLOTS),
                w4_raw[:, a, :].bitcast(U16).rearrange("p (m t) -> p t m", t=SLOTS),
            )
        load_table(2)

        stationary = ctx.enter_context(tc.tile_pool(name="stationary", bufs=1))
        pitch = H * 4 + H + 256

        v2_picked = keep.tile([P, S2], U32, name="v2_picked", align_bytes=64)
        v2_codes = stationary.tile([P, S2], U32, name="v2_codes", offset=PASSES * pitch + 128, align_bytes=64)
        v2_sc_picked = keep.tile([P, S2], U8, name="v2_sc_picked", align_bytes=64)
        v2_sc_dealt = keep.tile([P, S2], U8, name="v2_sc_dealt", align_bytes=64)
        nc.vector.tensor_copy(v2_sc_picked[:], tab2_sc[:].indirect(idx2[:]))
        nc.vector.tensor_copy(
            v2_sc_dealt[:].rearrange("p (g t m) -> p g t m", g=GROUPS, t=SLOTS),
            v2_sc_picked[:].rearrange("p (g m t) -> p g t m", g=GROUPS, t=SLOTS),
        )

        runs = [HALF] * (PASSES - 1) + [QUARTER]
        v_codes = [
            [keep.tile([P, runs[a]], U32, name="v_codes%d_%d" % (a, u), align_bytes=64) for u in range(S // runs[a])]
            for a in range(PASSES)
        ]

        def picked(a, n0, width):
            u, at = divmod(n0, runs[a])
            return v_codes[a][u][:, at : at + width].bitcast(FP8X4)

        gate_banks = [psum.tile([P, 2, QUARTER], F32, name="b%d" % c, tag="bank%d" % c) for c in range(BANKS)]
        for a in range(PASSES):
            run_cols = runs[a] // LIST_ROWS
            for u in range(S // runs[a]):
                nc.vector.tensor_copy(v_codes[a][u][:], tab_w[a][:].indirect(idx[:, u * run_cols : (u + 1) * run_cols]))
            if a == 0:
                load_table(PASSES - 1)
                nc.vector.tensor_copy(v2_picked[:], tab2_w[:].indirect(idx2[:]))
                nc.vector.tensor_copy(
                    v2_codes[:].bitcast(I32).rearrange("p (g t b i) -> p g b t i", g=GROUPS, t=SLOTS, i=PACK),
                    v2_picked[:].bitcast(I32).rearrange("p (g b i t) -> p g b t i", g=GROUPS, t=SLOTS, i=PACK),
                )
            if a in (1, 2):
                load_w1(2 * a - 2)
                load_w1(2 * a - 1)
            for c in range(BANKS):
                quarter, pair = divmod(c, 2)
                for s in range(2):
                    t = 2 * pair + s
                    nc.tensor.matmul_mx(
                        out=gate_banks[c][:, s, :],
                        lhsT=w4_codes[a][:, 2 * P * t : 2 * P * (t + 1)].bitcast(FP4X4),
                        lhsT_scale=planes[:, a, S + P * t : S + P * (t + 1)],
                        rhs=picked(a, quarter * QUARTER, QUARTER),
                        rhs_scale=planes[:, a, quarter * QUARTER : (quarter + 1) * QUARTER],
                        start=(a == 0 and s == 0),
                        stop=(a == PASSES - 1 and s == 1),
                    )

        nc.vector.memset(v2_plane[:].bitcast(I32), 0)
        for r in range(QUAD_ROWS):
            nc.sync.dma_start(
                v2_plane[r:P:QUAD, :].bitcast(I32), v2_sc_dealt[P - PLANE_ROWS + r : P : QUAD_ROWS, :].bitcast(I32)
            )
        nc.sync.dma_start(bias[:], bn.rearrange("(g p t) -> p g t", g=GROUPS, t=SLOTS))
        nc.sync.dma_start(gains[:], gain.rearrange("(g p t) -> p g t", g=GROUPS, t=SLOTS))

        gates = [keep.tile([P, SLOTS, HALF], F32, name="gate%d" % u) for u in range(2)]
        for c in range(BANKS):
            quarter, pair = divmod(c, 2)
            u, n0 = divmod(quarter * QUARTER, HALF)
            nc.scalar.activation(gates[u][:, 2 * pair : 2 * pair + 2, n0 : n0 + QUARTER], gate_banks[c][:], ACT.Sigmoid)

        w1_codes = [
            stationary.tile([P, H], U32, name="w1_codes%d" % a, offset=a * pitch + 128 + H, align_bytes=64) for a in range(PASSES)
        ]
        w1_planes = [stationary.tile([P, H], U8, name="w1_plane%d" % a, offset=a * pitch + 64, align_bytes=64) for a in range(PASSES)]
        for a in range(PASSES):
            w1_bf = ring.tile([P, H * PACK], BF16, name="woven", align_bytes=64)
            dealt = w1_bf[:].rearrange("p (t m j) -> p m j t", t=SLOTS, j=PACK)
            if a < PASSES - 2:
                whole = w1_raw[a][:].rearrange("p j (m t) -> p m j t", t=SLOTS)
                for u in range(2):
                    nc.vector.tensor_copy(dealt[:, :, :, 2 * u : 2 * u + 2], whole[:, :, :, 2 * u : 2 * u + 2])
            elif a == PASSES - 2:
                whole = w1_raw[a][:].rearrange("p j (m t) -> p m j t", t=SLOTS)
                nc.vector.tensor_copy(dealt[:, 0:THIRD_VECTOR], whole[:, 0:THIRD_VECTOR])
                nc.scalar.copy(dealt[:, THIRD_VECTOR:], whole[:, THIRD_VECTOR:])
            else:
                halves = [w1_last[u][:].rearrange("p j (m t) -> p m j t", t=SLOTS) for u in range(2)]
                nc.scalar.copy(dealt[:, 0 : P // 2], halves[0])
                nc.vector.tensor_copy(dealt[:, P // 2 :, :, 0:2], halves[1][:, :, :, 0:2])
                nc.scalar.copy(dealt[:, P // 2 :, :, 2:SLOTS], halves[1][:, :, :, 2:SLOTS])
            calls = 1 if a == PASSES - 2 else 2
            for u in range(calls):
                cols = slice(u * H // calls, (u + 1) * H // calls)
                nc.vector.quantize_mx(
                    out=w1_codes[a][:, cols].bitcast(FP8X4),
                    scales=w1_planes[a][:, cols],
                    in_=w1_bf[:, u * H * PACK // calls : (u + 1) * H * PACK // calls],
                )

        late = ctx.enter_context(tc.tile_pool(name="late", bufs=1))
        proj_banks = [psum.tile([P, SLOTS, TOK], F32, name="a%d" % c, tag="bank%d" % c) for c in range(BANKS)]
        starts = [sum(CHUNKS[:ci]) for ci in range(len(CHUNKS))]
        chunk_banks = [range(m0 // TOK, (m0 + width) // TOK) for m0, width in zip(starts, CHUNKS)]

        early = range(2)

        def project(a, banks, slots=range(SLOTS)):
            for c in banks:
                first_pass = 0 if c < FREED_EARLY else 1
                last_pass = PASSES - 1 if c in early else PASSES - 2
                for t in slots:
                    nc.tensor.matmul_mx(
                        out=proj_banks[c][:, t, :],
                        lhsT=w1_codes[a][:, P * t : P * (t + 1)].bitcast(FP8X4),
                        lhsT_scale=w1_planes[a][:, P * t : P * (t + 1)],
                        rhs=picked(a, c * TOK, TOK),
                        rhs_scale=planes[:, a, c * TOK : (c + 1) * TOK],
                        start=(a == first_pass and t == 0),
                        stop=(a == last_pass and t == SLOTS - 1),
                    )

        for banks in (early, range(len(early), FREED_EARLY)):
            project(0, banks, FIRST_PAIR)
            project(0, banks, SECOND_PAIR)
        project(1, range(BANKS), FIRST_PAIR)
        project(1, range(BANKS), SECOND_PAIR)
        project(0, range(FREED_EARLY, BANKS))
        project(2, early)
        project(3, early, FIRST_PAIR)
        project(3, early, SECOND_PAIR)

        def finish(banks):
            for c in banks:
                project(3, [c])
                project(2, [c])

        h_bf = late.tile([P, S * PACK], BF16, name="h_bf", align_bytes=64)
        h_codes = late.tile([P, S], U32, name="h_codes", align_bytes=64)
        h_plane = late.tile([P, S], U8, name="h_plane", align_bytes=64)

        def hidden(ci):
            for c in chunk_banks[ci]:
                u, n0 = divmod(c * TOK, HALF)
                nc.vector.tensor_tensor(
                    h_bf[:, c * TOK * PACK : (c + 1) * TOK * PACK].rearrange("p (n i t) -> p n t i", t=SLOTS, i=2),
                    proj_banks[c][:].rearrange("p t (n i) -> p n t i", i=2),
                    gates[u][:, :, n0 : n0 + TOK].rearrange("p t (n i) -> p n t i", i=2),
                    MULT,
                )
            m0, width = starts[ci], CHUNKS[ci]
            nc.vector.quantize_mx(
                out=h_codes[:, m0 : m0 + width].bitcast(FP8X4),
                scales=h_plane[:, m0 : m0 + width],
                in_=h_bf[:, m0 * PACK : (m0 + width) * PACK],
            )

        y = [late.tile([P, SLOTS, S], F32, name="y%d" % g, align_bytes=64) for g in range(GROUPS)]
        y_codes = [late.tile([P, S], U32, name="y_codes%d" % g, align_bytes=64) for g in range(GROUPS)]
        y_planes = late.tile([P, GROUPS, S], U8, name="y_planes", align_bytes=64)
        rows_out = [out_0[K_PASS * g : K_PASS * (g + 1), :].rearrange("(p t) m -> p t m", t=SLOTS) for g in range(GROUPS)]

        def neurons(g, m0, width, bank0):
            per_bank = BANK_F32 // width
            cols = slice(m0, m0 + width)
            for t0 in range(0, SLOTS, per_bank):
                z = psum.tile([P, per_bank, width], F32, name="z%d_%d_%d" % (g, m0, t0), tag="bank%d" % (bank0 + t0 // per_bank))
                for s in range(per_bank):
                    col = K_PASS * g + P * (t0 + s)
                    nc.tensor.matmul_mx(
                        out=z[:, s, :],
                        lhsT=v2_codes[:, col : col + P].bitcast(FP8X4),
                        lhsT_scale=v2_plane[:, col : col + P],
                        rhs=h_codes[:, cols].bitcast(FP8X4),
                        rhs_scale=h_plane[:, cols],
                        start=True,
                        stop=True,
                    )
                for s in range(per_bank):
                    t = t0 + s
                    nc.scalar.activation(y[g][:, t, cols], z[:, s, :], ACT.Gelu_apprx_tanh, bias=bias[:, g, t : t + 1])

        def scale(g, m0, width, pool_gains=0, slots=range(SLOTS)):
            cols = slice(m0, m0 + width)
            for t in slots:
                if t < pool_gains:
                    nc.gpsimd.tensor_scalar(y[g][:, t, cols], y[g][:, t, cols], gains[:, g, t : t + 1], 0.0, MULT, ADD)
                else:
                    nc.vector.tensor_scalar(y[g][:, t, cols], y[g][:, t, cols], gains[:, g, t : t + 1], None, MULT)
                if t % 2 == 1:
                    nc.sync.dma_start(rows_out[g][:, t - 1 : t + 1, cols], y[g][:, t - 1 : t + 1, cols])

        def round_y(g, m0, width, scalar_pairs):
            y_bf = ring.tile([P, width * PACK], BF16, name="woven", align_bytes=64)
            woven = y_bf[:].rearrange("p (n i t) -> p n t i", t=SLOTS, i=2)
            apart = y[g][:, :, m0 : m0 + width].rearrange("p t (n i) -> p n t i", i=2)
            if scalar_pairs > 0:
                nc.scalar.copy(woven[:, 0:scalar_pairs], apart[:, 0:scalar_pairs])
            if scalar_pairs < width // 2:
                nc.vector.tensor_copy(woven[:, scalar_pairs:], apart[:, scalar_pairs:])
            return y_bf

        def quantize_y(g, m0, width, span, y_bf):
            nc.vector.quantize_mx(
                out=y_codes[g][:, m0 : m0 + width].bitcast(FP8X4), scales=y_planes[:, g, m0 : m0 + width], in_=y_bf[:]
            )
            if (m0 + width) % span == 0:
                lo = m0 + width - span
                nc.sync.dma_start(
                    out_1[g].rearrange("p m t -> p (m t)")[:, PACK * lo : PACK * (lo + span)].bitcast(I32),
                    y_codes[g][:, lo : lo + span].bitcast(I32),
                )

        done = len(early)
        for ci, ahead in enumerate(BEFORE_NEURONS):
            finish(range(done, ahead))
            done = ahead
            if starts[ci] == QUARTER:
                scale(0, 0, QUARTER, POOL_GAINS)
            hidden(ci)
            neurons(0, starts[ci], CHUNKS[ci], chunk_banks[ci][0])
        finish(range(done, BANKS))

        scale(0, QUARTER, QUARTER)
        neurons(1, 0, HALF, 0)
        scale(1, 0, HALF, slots=FIRST_PAIR)
        hidden(len(CHUNKS) - 1)
        neurons(0, HALF, HALF, BANKS // 2)
        neurons(1, HALF, HALF, 0)
        scale(1, 0, HALF, slots=SECOND_PAIR)
        scale(0, HALF, HALF)
        scale(1, HALF, HALF)

        pieces = [
            (0, 0, QUARTER, HALF, 0),
            (0, QUARTER, QUARTER, HALF, 0),
            (1, 0, HALF, HALF, 0),
            (0, HALF, HALF, HALF, SCALAR_PAIRS[0]),
            (1, HALF, QUARTER, QUARTER, SCALAR_PAIRS[1]),
            (1, HALF + QUARTER, QUARTER, QUARTER, SCALAR_PAIRS[2]),
        ]
        waiting = None
        for g, m0, width, span, scalar_pairs in pieces:
            y_bf = round_y(g, m0, width, scalar_pairs)
            if waiting is not None:
                quantize_y(*waiting)
            waiting = (g, m0, width, span, y_bf)
        quantize_y(*waiting)
        for r in range(QUAD_ROWS):
            (nc.scalar, nc.sync)[r % 2].dma_start(
                out_2[:, r::QUAD_ROWS, :].rearrange("g q m -> q g m").bitcast(I32), y_planes[r:P:QUAD, :, :].bitcast(I32)
            )
